import numpy as np
import ml_dtypes


def mxq(x, axis, fmt="e4m3"):
    dtype, down = {"e4m3": (ml_dtypes.float8_e4m3fn, 7), "e5m2": (ml_dtypes.float8_e5m2, 14)}[fmt]
    v = np.moveaxis(np.asarray(x, np.float32).astype(ml_dtypes.bfloat16).astype(np.float64), axis, -1)
    blocks = v.reshape(v.shape[:-1] + (-1, 32))
    amax = np.abs(blocks).max(-1, keepdims=True)
    byte = np.maximum(np.where(amax > 0, np.frexp(amax)[1] - 1 + 127, 0) - down, 1)
    scale = np.exp2(byte - 127.0)
    codes = (blocks / scale).astype(np.float32).astype(dtype).astype(np.float64)
    return np.moveaxis((codes * scale).reshape(v.shape), -1, axis)


WIDE = False


def mx_kscale(k):
    if not WIDE:
        return np.ones(k)
    levels = np.array([10, -10, 5, -5, 0])
    if k % 512:
        return np.exp2(np.random.permutation(np.resize(levels, k // 32))).repeat(32)
    a = np.empty((k // 512, 16))
    for p in range(k // 512):
        a[p, :8] = np.random.permutation(np.resize(levels, 8))
        for g in range(8):
            far = levels[np.abs(levels - a[p, g]) >= 10]
            a[p, g + 8] = far[np.random.randint(len(far))]
    return np.exp2(a.ravel()).repeat(32)


def f64(x):
    return np.asarray(x).astype(np.float64)


def striped(idx):
    return np.tile(idx.reshape(-1, 16).T, (8, 1)).astype(np.uint16)


def unstriped(offs):
    return offs[:16].T.reshape(-1).astype(np.int64)


E2M1 = np.array([0.0, 0.5, 1.0, 1.5, 2.0, 3.0, 4.0, 6.0, -0.0, -0.5, -1.0, -1.5, -2.0, -3.0, -4.0, -6.0])


def pack_weight(w, fmt):
    k, n = w.shape
    w = f64(np.asarray(w, np.float32).astype(ml_dtypes.bfloat16)).reshape(k // 32, 32, n)
    amax = np.abs(w).max(1)
    if fmt == "e4m3":
        byte = np.frexp(amax)[1] - 1 + 127 - 7
    else:
        mant, ex = np.frexp(amax / 6.0)
        byte = np.where(mant > 0.5, ex, ex - 1) + 127
    byte = np.clip(np.where(amax > 0, byte, 1), 1, 254)
    scaled = (w * np.exp2(127.0 - byte)[:, None, :]).reshape(k, n).astype(np.float32)
    by_word = np.ascontiguousarray(scaled.reshape(k // 512, 128, 4, n).transpose(0, 1, 3, 2))
    if fmt == "e4m3":
        words = by_word.astype(ml_dtypes.float8_e4m3fn).view(np.uint8)
    else:
        c = by_word.astype(ml_dtypes.float4_e2m1fn).view(np.uint8) & 0xF
        words = (c[..., 0::2] | (c[..., 1::2] << 4)).reshape(k // 512, 128, 2 * n)
    return np.ascontiguousarray(words), np.ascontiguousarray(byte.astype(np.uint8).reshape(k // 512, 16, n))


def unpack_weight(words, scales, fmt):
    g, _, n = scales.shape
    words = np.ascontiguousarray(words).reshape(g, 128, n, -1)
    if fmt == "e4m3":
        vals = words.view(ml_dtypes.float8_e4m3fn).astype(np.float64)
    else:
        nib = np.empty((g, 128, n, 4), np.uint8)
        nib[..., 0::2] = words & 0xF
        nib[..., 1::2] = words >> 4
        vals = E2M1[nib]
    vals = vals * np.repeat(np.exp2(scales.astype(np.float64) - 127.0), 8, axis=1)[..., None]
    return vals.transpose(0, 1, 3, 2).reshape(g * 512, n)


def relu(v):
    return np.maximum(v, 0.0)


K, T, E, C, H, N, HOT = 1024, 512, 8, 256, 512, 256, 4
TOP = 4


def by_expert(wq, xq):
    return np.concatenate([wq[e].T @ xq[:, e * C:(e + 1) * C] for e in range(E)], axis=1)


def setup_inputs():
    n = np.random.standard_normal
    s = mx_kscale(K)
    u = mx_kscale(H)
    deal = np.repeat(np.arange(E), C).reshape(TOP, T)[:, np.random.permutation(T)]
    deal = np.take_along_axis(deal, np.argsort(np.random.rand(TOP, T), axis=0), axis=0)
    for _ in range(8):
        s_, t_ = np.random.permutation(T).reshape(2, -1); r = np.random.randint(TOP, size=T // 2); x, y = deal[r, s_].copy(), deal[r, t_].copy()
        ok = ~((deal[:, s_] == y).any(0) | (deal[:, t_] == x).any(0)); deal[r[ok], s_[ok]] = y[ok]; deal[r[ok], t_[ok]] = x[ok]
    order = np.lexsort((np.random.rand(TOP * T), deal.reshape(-1)))
    slot_token = order % T; pos = np.empty(TOP * T, np.int64); pos[order] = np.arange(TOP * T); pos = pos.reshape(TOP, T)
    g = np.random.uniform(0.5, 1.5, (TOP, T)); g = g / g.sum(0)
    x = pack_weight(n((K, T)) * s[:, None], "e4m3")
    w1h = [pack_weight(m, "e4m3") for m in n((HOT, K, H)) / np.sqrt(K) / s[None, :, None] * u]
    w2h = [pack_weight(m, "e4m3") for m in n((HOT, H, N)) / np.sqrt(H) / u[None, :, None]]
    w1c = [pack_weight(m, "e2m1") for m in n((E - HOT, K, H)) / np.sqrt(K) / s[None, :, None] * u]
    w2c = [pack_weight(m, "e2m1") for m in n((E - HOT, H, N)) / np.sqrt(H) / u[None, :, None]]
    return {
        "x_words": x[0],
        "x_scales": x[1],
        "w1h_words": np.stack([m[0] for m in w1h]),
        "w1h_scales": np.stack([m[1] for m in w1h]),
        "w2h_words": np.stack([m[0] for m in w2h]),
        "w2h_scales": np.stack([m[1] for m in w2h]),
        "w1c_words": np.stack([m[0] for m in w1c]),
        "w1c_scales": np.stack([m[1] for m in w1c]),
        "w2c_words": np.stack([m[0] for m in w2c]),
        "w2c_scales": np.stack([m[1] for m in w2c]),
        "gate": np.stack([np.tile(r, (128, 1)) for r in g]).astype(np.float32),
        "offs": striped(slot_token),
        "pos1": striped(pos[0]),
        "pos2": striped(pos[1]),
        "pos3": striped(pos[2]),
        "pos4": striped(pos[3]),
    }


def reference(x_words, x_scales, w1h_words, w1h_scales, w2h_words, w2h_scales, w1c_words, w1c_scales, w2c_words, w2c_scales, gate, offs, pos1, pos2, pos3, pos4):
    w1h = np.stack([unpack_weight(w1h_words[e], w1h_scales[e], "e4m3") for e in range(HOT)])
    w2h = np.stack([unpack_weight(w2h_words[e], w2h_scales[e], "e4m3") for e in range(HOT)])
    w1c = np.stack([unpack_weight(w1c_words[e], w1c_scales[e], "e2m1") for e in range(E - HOT)])
    w2c = np.stack([unpack_weight(w2c_words[e], w2c_scales[e], "e2m1") for e in range(E - HOT)])
    idx = unstriped(offs)
    xq = unpack_weight(x_words, x_scales, "e4m3")[:, idx]
    w1 = [*w1h, *w1c]
    w2 = [*w2h, *w2c]
    h = relu(by_expert(w1, xq))
    y = by_expert(w2, mxq(h, 0, "e4m3"))
    out = sum(f64(gate[r, :1]) * y[:, unstriped(p)] for r, p in enumerate((pos1, pos2, pos3, pos4)))
    return out

@@ -1,0 +1,283 @@
+from contextlib import ExitStack
+
+import concourse.mybir as mybir
+from concourse.masks import make_identity
+
+K, T, E, C, H, N, HOT, TOP = 1024, 512, 8, 256, 512, 256, 4, 4
+S = E * C
+P = 128
+FLOPS = 2 * S * (K * H + H * N)
+
+F32 = mybir.dt.float32
+BF16 = mybir.dt.bfloat16
+I32 = mybir.dt.int32
+U32 = mybir.dt.uint32
+U16 = mybir.dt.uint16
+U8 = mybir.dt.uint8
+FP8X4 = mybir.dt.float8_e4m3fn_x4
+FP4X4 = mybir.dt.float4_e2m1fn_x4
+RELU = mybir.ActivationFunctionType.Relu
+MULT = mybir.AluOpType.mult
+ADD = mybir.AluOpType.add
+
+
+def tile_moe_hot_mlp_relu_kernel(
+    tc, x_words, x_scales, w1h_words, w1h_scales, w2h_words, w2h_scales,
+    w1c_words, w1c_scales, w2c_words, w2c_scales, gate, offs, pos1, pos2, pos3, pos4, out,
+):
+    nc = tc.nc
+    with ExitStack() as ctx:
+        lists = ctx.enter_context(tc.tile_pool(name="lists", bufs=1))
+        keep = ctx.enter_context(tc.tile_pool(name="keep", bufs=1))
+        ring = ctx.enter_context(tc.tile_pool(name="ring", bufs=2))
+        work = ctx.enter_context(tc.tile_pool(name="work", bufs=3))
+        ps_h = ctx.enter_context(tc.psum_pool(name="ps_h", bufs=4))
+        ps_t = ctx.enter_context(tc.psum_pool(name="ps_t", bufs=2))
+        ps_y = ctx.enter_context(tc.psum_pool(name="ps_y", bufs=2))
+
+        def kept(shape, dtype, name, tag=None):
+            return keep.tile(shape, dtype, name=name, tag=tag or name, align_bytes=64)
+
+        offs_t = lists.tile([P, S // 16], U16, name="offs_t")
+        pos_t = [lists.tile([P, T // 16], U16, name=f"pos_t{r}") for r in range(TOP)]
+        xw = kept([P, 2, T], U32, "xw")
+        xs = kept([P, T], U8, "xs")
+        w1 = [kept([P, 2, H], U32, f"w1_{e}") if e < HOT else kept([P, 2, 2 * H], U8, f"w1_{e}")
+              for e in range(E)]
+        s1h = [kept([P, H], U8, f"s1h{g}") for g in range(HOT // 2)]
+        s1c = kept([P, 2 * (E - HOT), H], U8, "s1c")
+        s2h = kept([P, HOT, N], U8, "s2h")
+        s2c = kept([P, E - HOT, N], U8, "s2c")
+        moved = kept([P, E - HOT, C], U8, "moved")
+        ident0 = kept([P, P], F32, "ident0")
+        ident = kept([P, P], F32, "ident")
+
+        def as_words(tile3):
+            return tile3[:].rearrange("p a b -> p (a b)").bitcast(I32)
+
+        nc.vector.memset(xs[:].bitcast(I32), 0)
+        for g in range(HOT // 2):
+            nc.vector.memset(s1h[g][:].bitcast(I32), 0)
+        make_identity(nc, ident0[:])
+        nc.scalar.activation(ident[:], ident0[:], RELU)
+        for plane in (s1c, moved, s2h, s2c):
+            nc.gpsimd.memset(as_words(plane), 0)
+
+        def load_planes(tile3, scales):
+            src = scales.bitcast(I32).rearrange("e s (q r) n -> r q (e s) n", r=4)
+            dst = tile3[:].bitcast(I32)
+            for r in range(4):
+                nc.sync.dma_start(out=dst[r:P:32], in_=src[r])
+
+        def load_w1(e):
+            if e < HOT:
+                src = w1h_words[e].rearrange("s p i d -> p s (i d)")
+            else:
+                src = w1c_words[e - HOT].rearrange("s p b -> p s b")
+            nc.sync.dma_start(out=w1[e][:].bitcast(I32), in_=src.bitcast(I32))
+
+        s1h_src = w1h_scales.bitcast(I32).rearrange("(g a) s b n -> g (a s) b n", a=2)
+
+        def load_packed(g, queue):
+            for q in range(4):
+                queue.dma_start(out=s1h[g][:].bitcast(I32)[32 * q:32 * q + 16],
+                                in_=s1h_src[g, :, 4 * q:4 * q + 4, :])
+
+        nc.sync.dma_start(offs_t[:], offs)
+        for q in range(4):
+            nc.sync.dma_start(out=xs[:].bitcast(I32)[32 * q:32 * q + 8],
+                                in_=x_scales.bitcast(I32)[:, 4 * q:4 * q + 4, :])
+        nc.sync.dma_start(out=xw[:].bitcast(I32),
+                          in_=x_words.rearrange("s p t d -> p s (t d)").bitcast(I32))
+        load_w1(0)
+        load_packed(0, nc.sync)
+        load_w1(1)
+        load_w1(2)
+        load_packed(1, nc.sync)
+        load_w1(3)
+        load_planes(s1c, w1c_scales)
+        for e in range(HOT, E):
+            load_w1(e)
+
+        gw, gs = {}, {}
+
+        def gather_words(e, pieces=1):
+            for s in range(2):
+                gw[e, s] = ring.tile([P, C], U32, name=f"gw{s}", align_bytes=64)
+            width = C // pieces
+            for j in range(pieces):
+                first = (e * C + j * width) // 16
+                for s in range(2):
+                    nc.vector.tensor_copy(gw[e, s][:, j * width:(j + 1) * width],
+                                          xw[:, s, :].indirect(offs_t[:, first:first + width // 16]))
+
+        gs_tag = ["gs_a", "gs_a", "w1_0", "gs_a", "w1_1", "w1_0", "gs_a", "w1_1"]
+
+        def gather_scales(e):
+            gs[e] = kept([P, C], U8, f"gs{e}", gs_tag[e])
+            nc.vector.tensor_copy(gs[e][:], xs[:].indirect(offs_t[:, e * C // 16:(e + 1) * C // 16]))
+            if e >= HOT:
+                for r in range(4):
+                    nc.sync.dma_start(out=moved[:, e - HOT, :].bitcast(I32)[r:P:32],
+                                      in_=gs[e][:].bitcast(I32)[4 + r:P:32])
+
+        hb, hq, hc, hs = {}, {}, {}, {}
+        y = [kept([P, S], F32, f"y{half}") for half in range(2)]
+
+        def layer1(e):
+            for j in range(2):
+                cols = slice(j * P, (j + 1) * P)
+                acc = ps_h.tile([P, H], F32, name="acc")
+                for s in range(2):
+                    if e < HOT:
+                        w, ws = w1[e][:, s, :].bitcast(FP8X4), s1h[e // 2][4 * (2 * (e % 2) + s):P]
+                        ts = gs[e][4 * s:P, cols]
+                    else:
+                        w, ws = w1[e][:, s, :].bitcast(FP4X4), s1c[:, 2 * (e - HOT) + s, :]
+                        ts = gs[e][:, cols] if s == 0 else moved[:, e - HOT, cols]
+                    nc.tensor.matmul_mx(out=acc[:], lhsT=gw[e, s][:, cols].bitcast(FP8X4),
+                                        lhsT_scale=ts, rhs=w, rhs_scale=ws,
+                                        start=(s == 0), stop=(s == 1))
+                hb[e, j] = work.tile([P, H], BF16, name="hb", bufs=4, align_bytes=64)
+                dst = hb[e, j][:].rearrange("m (u p d) -> m u p d", u=2, d=2)
+                src = acc[:].rearrange("m (p u d) -> m u p d", u=2, d=2)
+                if (e, j) == (E - 1, 1):
+                    nc.vector.tensor_scalar_max(dst, src, 0.0)
+                else:
+                    nc.scalar.activation(dst, src, RELU)
+
+        def turn(e):
+            if e % 2 == 0:
+                hq[e // 2] = kept([P, 2, 4 * C], BF16, f"hq{e // 2}")
+            dst = hq[e // 2][:, e % 2, :].bitcast(F32).rearrange("p (j m u) -> p j m u", j=2, u=2)
+            if e < E - 1:
+                bank = ps_t.tile([P, 2, 2, P], F32, name="bank")
+                for j in range(2):
+                    for u in range(2):
+                        nc.tensor.transpose(bank[:, j, u, :],
+                                            hb[e, j][:].bitcast(F32)[:, u * P:(u + 1) * P], ident[:])
+                nc.scalar.copy(dst, bank[:].rearrange("p j u m -> p j m u"))
+            else:
+                for j in range(2):
+                    bank = ps_t.tile([P, 2, P], F32, name="bank")
+                    for u in range(2):
+                        nc.tensor.transpose(bank[:, u, :],
+                                            hb[e, j][:].bitcast(F32)[:, u * P:(u + 1) * P], ident[:])
+                    if j == 0:
+                        nc.scalar.copy(dst[:, j], bank[:].rearrange("p u m -> p m u"))
+                    else:
+                        nc.vector.tensor_copy(dst[:, j], bank[:].rearrange("p u m -> p m u"))
+
+        def quantise(pair):
+            if pair < 3:
+                hc[pair] = ring.tile([P, 2 * C], U32, name=f"hc{pair}", tag=f"gw{pair % 2}", align_bytes=64)
+            else:
+                hc[pair] = kept([P, 2 * C], U32, f"hc{pair}")
+            hs[pair] = kept([P, 2 * C], U8, f"hs{pair}")
+            if pair < 3:
+                nc.vector.quantize_mx(out=hc[pair][:].bitcast(FP8X4), scales=hs[pair][:],
+                                      in_=hq[pair][:].rearrange("p a b -> p (a b)"))
+            else:
+                for a in range(2):
+                    nc.vector.quantize_mx(out=hc[pair][:, a * C:(a + 1) * C].bitcast(FP8X4),
+                                          scales=hs[pair][:, a * C:(a + 1) * C], in_=hq[pair][:, a, :])
+
+        late = {}
+
+        def layer2(experts, half, engine):
+            acc = ps_y.tile([P, len(experts), C], F32, name="accy")
+            cols = slice(half * P, (half + 1) * P)
+            for j, e in enumerate(experts):
+                if e < HOT:
+                    w, ws = late["w2h"][:, e, cols].bitcast(FP8X4), s2h[:, e, cols]
+                else:
+                    w = late["w2c"][:, e - HOT, 2 * half * P:2 * (half + 1) * P].bitcast(FP4X4)
+                    ws = s2c[:, e - HOT, cols]
+                mine = slice((e % 2) * C, (e % 2 + 1) * C)
+                nc.tensor.matmul_mx(out=acc[:, j, :], lhsT=w, lhsT_scale=ws,
+                                    rhs=hc[e // 2][:, mine].bitcast(FP8X4), rhs_scale=hs[e // 2][:, mine],
+                                    start=True, stop=True)
+            dst = y[half][:, experts[0] * C:(experts[-1] + 1) * C]
+            src = acc[:].rearrange("p j c -> p (j c)")
+            if engine == "s":
+                nc.scalar.copy(dst, src)
+            else:
+                nc.vector.tensor_copy(dst, src)
+
+        def late_load(e):
+            if e == 5:
+                late["w2h"] = kept([P, HOT, N], U32, "w2h", f"w1_{e}")
+                nc.sync.dma_start(out=late["w2h"][:].bitcast(I32),
+                                  in_=w2h_words.rearrange("e s p n d -> p (e s) (n d)").bitcast(I32))
+            elif e == 4:
+                late["w2c"] = kept([P, E - HOT, 2 * N], U8, "w2c", f"w1_{e}")
+                nc.sync.dma_start(out=late["w2c"][:].bitcast(I32),
+                                  in_=w2c_words.rearrange("e s p b -> p (e s) b").bitcast(I32))
+            elif e >= 6:
+                late[e - 6] = kept([P, 2, T], F32, f"gate{e}", f"w1_{e}")
+                nc.sync.dma_start(out=late[e - 6][:],
+                                  in_=gate[2 * (e - 6):2 * (e - 5)].rearrange("r p t -> p r t"))
+
+        gather_scales(0)
+        gather_words(0, 2)
+        gather_words(1)
+        for e in range(E):
+            layer1(e)
+            if e == 0:
+                gather_scales(1)
+            if HOT <= e + 3 < E:
+                gather_scales(e + 3)
+            if e + 2 < E:
+                gather_words(e + 2)
+            if e + 2 < HOT:
+                gather_scales(e + 2)
+            late_load(e)
+            if e == 2:
+                load_planes(s2h, w2h_scales)
+                load_planes(s2c, w2c_scales)
+                for r, pos in enumerate((pos1, pos2, pos3, pos4)):
+                    nc.sync.dma_start(pos_t[r][:], pos)
+            if e >= 1:
+                turn(e - 1)
+        turn(E - 1)
+        for pair in range(4):
+            quantise(pair)
+        layer2([0, 1], 0, "s")
+        layer2([2, 3], 0, "v")
+        layer2([4, 5], 0, "s")
+        layer2([6], 0, "s")
+        layer2([7], 0, "v")
+        for pair in range(E // 2):
+            layer2([2 * pair, 2 * pair + 1], 1, "s")
+
+        prod = {}
+
+        def fetch(half, r):
+            prod[half, r] = kept([P, T], F32, f"prod{half}_{r}")
+            nc.vector.tensor_tensor(prod[half, r][:], y[half][:].indirect(pos_t[r][:]),
+                                    late[r // 2][:, r % 2, :], MULT)
+
+        part = {}
+
+        def add_three(half):
+            bank = ps_t.tile([P, 4, P], F32, name="bank")
+            for c in range(4):
+                for r in range(3):
+                    nc.tensor.matmul(bank[:, c, :], lhsT=prod[half, r][:, c * P:(c + 1) * P],
+                                     rhs=ident[:], start=(r == 0), stop=(r == 2), is_transpose=True)
+            turned = work.tile([P, 4, P], F32, name="turned")
+            nc.scalar.copy(turned[:], bank[:])
+            part[half] = ps_h.tile([P, T], F32, name="acc")
+            for c in range(4):
+                nc.tensor.transpose(part[half][:, c * P:(c + 1) * P], turned[:, c, :], ident[:])
+
+        for half in range(2):
+            for r in range(3):
+                fetch(half, r)
+            add_three(half)
+        for half in range(2):
+            fetch(half, 3)
+        for half in range(2):
+            res = work.tile([P, T], F32, name="res")
+            nc.vector.tensor_tensor(res[:], part[half][:], prod[half, 3][:], ADD)
+            nc.sync.dma_start(out=out[half * P:(half + 1) * P, :], in_=res[:])

@@ -29,11 +29,10 @@ def tile_moe_hot_mlp_relu_kernel(
     with ExitStack() as ctx:
         lists = ctx.enter_context(tc.tile_pool(name="lists", bufs=1))
         keep = ctx.enter_context(tc.tile_pool(name="keep", bufs=1))
-        ring = ctx.enter_context(tc.tile_pool(name="ring", bufs=2))
-        work = ctx.enter_context(tc.tile_pool(name="work", bufs=3))
-        ps_h = ctx.enter_context(tc.psum_pool(name="ps_h", bufs=4))
-        ps_t = ctx.enter_context(tc.psum_pool(name="ps_t", bufs=2))
-        ps_y = ctx.enter_context(tc.psum_pool(name="ps_y", bufs=2))
+        psum = ctx.enter_context(tc.psum_pool(name="psum", bufs=1))
+
+        def bank_tile(tag, shape, name):
+            return psum.tile(shape, F32, name=name, tag=tag)
 
         def kept(shape, dtype, name, tag=None):
             return keep.tile(shape, dtype, name=name, tag=tag or name, align_bytes=64)
@@ -56,18 +55,19 @@ def tile_moe_hot_mlp_relu_kernel(
             return tile3[:].rearrange("p a b -> p (a b)").bitcast(I32)
 
         nc.vector.memset(xs[:].bitcast(I32), 0)
-        for g in range(HOT // 2):
-            nc.vector.memset(s1h[g][:].bitcast(I32), 0)
+        nc.vector.memset(s1h[0][:].bitcast(I32), 0)
+        nc.vector.memset(as_words(s1c), 0)
+        nc.vector.memset(s1h[1][:].bitcast(I32), 0)
         make_identity(nc, ident0[:])
         nc.scalar.activation(ident[:], ident0[:], RELU)
-        for plane in (s1c, moved, s2h, s2c):
-            nc.gpsimd.memset(as_words(plane), 0)
+        for plane in (moved, s2h, s2c):
+            nc.vector.memset(as_words(plane), 0)
 
-        def load_planes(tile3, scales):
+        def load_planes(tile3, scales, queue):
             src = scales.bitcast(I32).rearrange("e s (q r) n -> r q (e s) n", r=4)
             dst = tile3[:].bitcast(I32)
             for r in range(4):
-                nc.sync.dma_start(out=dst[r:P:32], in_=src[r])
+                queue.dma_start(out=dst[r:P:32], in_=src[r])
 
         def load_w1(e):
             if e < HOT:
@@ -83,109 +83,103 @@ def tile_moe_hot_mlp_relu_kernel(
                 queue.dma_start(out=s1h[g][:].bitcast(I32)[32 * q:32 * q + 16],
                                 in_=s1h_src[g, :, 4 * q:4 * q + 4, :])
 
-        nc.sync.dma_start(offs_t[:], offs)
-        for q in range(4):
-            nc.sync.dma_start(out=xs[:].bitcast(I32)[32 * q:32 * q + 8],
-                                in_=x_scales.bitcast(I32)[:, 4 * q:4 * q + 4, :])
         nc.sync.dma_start(out=xw[:].bitcast(I32),
                           in_=x_words.rearrange("s p t d -> p s (t d)").bitcast(I32))
+        for q in range(4):
+            nc.sync.dma_start(out=xs[:].bitcast(I32)[32 * q:32 * q + 8],
+                              in_=x_scales.bitcast(I32)[:, 4 * q:4 * q + 4, :])
+        nc.sync.dma_start(offs_t[:], offs)
         load_w1(0)
         load_packed(0, nc.sync)
         load_w1(1)
         load_w1(2)
         load_packed(1, nc.sync)
         load_w1(3)
-        load_planes(s1c, w1c_scales)
-        for e in range(HOT, E):
-            load_w1(e)
+        load_planes(s1c, w1c_scales, nc.gpsimd)
 
         gw, gs = {}, {}
 
-        def gather_words(e, pieces=1):
-            for s in range(2):
-                gw[e, s] = ring.tile([P, C], U32, name=f"gw{s}", align_bytes=64)
-            width = C // pieces
-            for j in range(pieces):
-                first = (e * C + j * width) // 16
+        def gather_words(e):
+            tiles = [kept([P, C], U32, f"gw{e}_{s}") for s in range(2)]
+            width = P if e == 0 else C
+            for first in range(0, C, width):
+                entries = offs_t[:, (e * C + first) // 16:(e * C + first + width) // 16]
                 for s in range(2):
-                    nc.vector.tensor_copy(gw[e, s][:, j * width:(j + 1) * width],
-                                          xw[:, s, :].indirect(offs_t[:, first:first + width // 16]))
-
-        gs_tag = ["gs_a", "gs_a", "w1_0", "gs_a", "w1_1", "w1_0", "gs_a", "w1_1"]
+                    nc.vector.tensor_copy(tiles[s][:, first:first + width], xw[:, s, :].indirect(entries))
+            for s in range(2):
+                for j in range(2):
+                    gw[e, s, j] = tiles[s][:, j * P:(j + 1) * P]
 
         def gather_scales(e):
-            gs[e] = kept([P, C], U8, f"gs{e}", gs_tag[e])
+            gs[e] = kept([P, C], U8, f"gs{e}")
             nc.vector.tensor_copy(gs[e][:], xs[:].indirect(offs_t[:, e * C // 16:(e + 1) * C // 16]))
             if e >= HOT:
-                for r in range(4):
-                    nc.sync.dma_start(out=moved[:, e - HOT, :].bitcast(I32)[r:P:32],
-                                      in_=gs[e][:].bitcast(I32)[4 + r:P:32])
+                nc.sync.dma_start(out=moved[:, e - HOT, :].bitcast(I32)[0:112],
+                                  in_=gs[e][:].bitcast(I32)[4:116])
 
-        hb, hq, hc, hs = {}, {}, {}, {}
+        hb = {}
         y = [kept([P, S], F32, f"y{half}") for half in range(2)]
 
-        def layer1(e):
-            for j in range(2):
-                cols = slice(j * P, (j + 1) * P)
-                acc = ps_h.tile([P, H], F32, name="acc")
-                for s in range(2):
-                    if e < HOT:
-                        w, ws = w1[e][:, s, :].bitcast(FP8X4), s1h[e // 2][4 * (2 * (e % 2) + s):P]
-                        ts = gs[e][4 * s:P, cols]
-                    else:
-                        w, ws = w1[e][:, s, :].bitcast(FP4X4), s1c[:, 2 * (e - HOT) + s, :]
-                        ts = gs[e][:, cols] if s == 0 else moved[:, e - HOT, cols]
-                    nc.tensor.matmul_mx(out=acc[:], lhsT=gw[e, s][:, cols].bitcast(FP8X4),
-                                        lhsT_scale=ts, rhs=w, rhs_scale=ws,
-                                        start=(s == 0), stop=(s == 1))
-                hb[e, j] = work.tile([P, H], BF16, name="hb", bufs=4, align_bytes=64)
-                dst = hb[e, j][:].rearrange("m (u p d) -> m u p d", u=2, d=2)
-                src = acc[:].rearrange("m (p u d) -> m u p d", u=2, d=2)
-                if (e, j) == (E - 1, 1):
-                    nc.vector.tensor_scalar_max(dst, src, 0.0)
+        sums = {}
+
+        def layer1(e, j):
+            cols = slice(j * P, (j + 1) * P)
+            sums[e, j] = bank_tile(f"r{max(3 * e - 1 + j, j) % 4}", [P, H], f"sums{e}_{j}")
+            for s in range(2):
+                if e < HOT:
+                    w, ws = w1[e][:, s, :].bitcast(FP8X4), s1h[e // 2][4 * (2 * (e % 2) + s):P]
+                    ts = gs[e][4 * s:P, cols]
                 else:
-                    nc.scalar.activation(dst, src, RELU)
+                    w, ws = w1[e][:, s, :].bitcast(FP4X4), s1c[:, 2 * (e - HOT) + s, :]
+                    ts = gs[e][:, cols] if s == 0 else moved[:, e - HOT, cols]
+                nc.tensor.matmul_mx(out=sums[e, j][:], lhsT=gw[e, s, j].bitcast(FP8X4),
+                                    lhsT_scale=ts, rhs=w, rhs_scale=ws,
+                                    start=(s == 0), stop=(s == 1))
+
+        def relu(e, j):
+            hb[e, j] = kept([P, H], BF16, f"hb{e}_{j}")
+            dst = hb[e, j][:].rearrange("m (u p d) -> m u p d", u=2, d=2)
+            src = sums[e, j][:].rearrange("m (p u d) -> m u p d", u=2, d=2)
+            nc.scalar.activation(dst, src, RELU)
+
+        turned_h = {}
 
         def turn(e):
-            if e % 2 == 0:
-                hq[e // 2] = kept([P, 2, 4 * C], BF16, f"hq{e // 2}")
-            dst = hq[e // 2][:, e % 2, :].bitcast(F32).rearrange("p (j m u) -> p j m u", j=2, u=2)
-            if e < E - 1:
-                bank = ps_t.tile([P, 2, 2, P], F32, name="bank")
-                for j in range(2):
+            groups = [(f"r{3 * e % 4}", (0, 1))] if e < E - 1 else [("c0", (0,)), ("c1", (1,))]
+            for tag, js in groups:
+                bank = bank_tile(tag, [P, len(js), 2, P], f"turned_h{e}_{js[0]}")
+                for i, j in enumerate(js):
                     for u in range(2):
-                        nc.tensor.transpose(bank[:, j, u, :],
+                        nc.tensor.transpose(bank[:, i, u, :],
                                             hb[e, j][:].bitcast(F32)[:, u * P:(u + 1) * P], ident[:])
-                nc.scalar.copy(dst, bank[:].rearrange("p j u m -> p j m u"))
-            else:
-                for j in range(2):
-                    bank = ps_t.tile([P, 2, P], F32, name="bank")
-                    for u in range(2):
-                        nc.tensor.transpose(bank[:, u, :],
-                                            hb[e, j][:].bitcast(F32)[:, u * P:(u + 1) * P], ident[:])
-                    if j == 0:
-                        nc.scalar.copy(dst[:, j], bank[:].rearrange("p u m -> p m u"))
-                    else:
-                        nc.vector.tensor_copy(dst[:, j], bank[:].rearrange("p u m -> p m u"))
+                turned_h[e, js[0]] = bank
 
-        def quantise(pair):
-            if pair < 3:
-                hc[pair] = ring.tile([P, 2 * C], U32, name=f"hc{pair}", tag=f"gw{pair % 2}", align_bytes=64)
+        hq = [kept([P, 2, 4 * C], BF16, f"hq{pair}") for pair in range(E // 2)]
+        hc = [kept([P, 2, C], U32, f"hc{pair}") for pair in range(E // 2)]
+        hs = [kept([P, 2, C], U8, f"hs{pair}") for pair in range(E // 2)]
+
+        def interleave(e, j=0):
+            dst = hq[e // 2][:, e % 2, :].bitcast(F32).rearrange("p (j m u) -> p j m u", j=2, u=2)
+            src = turned_h[e, j][:].rearrange("p j u m -> p j m u")
+            if e < E - 1:
+                nc.scalar.copy(dst, src)
+            elif j == 0:
+                nc.scalar.copy(dst[:, 0:1], src)
             else:
-                hc[pair] = kept([P, 2 * C], U32, f"hc{pair}")
-            hs[pair] = kept([P, 2 * C], U8, f"hs{pair}")
-            if pair < 3:
-                nc.vector.quantize_mx(out=hc[pair][:].bitcast(FP8X4), scales=hs[pair][:],
-                                      in_=hq[pair][:].rearrange("p a b -> p (a b)"))
-            else:
-                for a in range(2):
-                    nc.vector.quantize_mx(out=hc[pair][:, a * C:(a + 1) * C].bitcast(FP8X4),
-                                          scales=hs[pair][:, a * C:(a + 1) * C], in_=hq[pair][:, a, :])
+                nc.vector.tensor_copy(dst[:, 1:2], src)
+
+        def quantise(experts):
+            pair, mine = experts[0] // 2, slice(experts[0] % 2, experts[-1] % 2 + 1)
+            nc.vector.quantize_mx(out=hc[pair][:, mine, :].rearrange("p a c -> p (a c)").bitcast(FP8X4),
+                                  scales=hs[pair][:, mine, :].rearrange("p a c -> p (a c)"),
+                                  in_=hq[pair][:, mine, :].rearrange("p a c -> p (a c)"))
 
         late = {}
 
-        def layer2(experts, half, engine):
-            acc = ps_y.tile([P, len(experts), C], F32, name="accy")
+        outs = {}
+
+        def layer2(experts, half, tag):
+            acc = bank_tile(tag, [P, len(experts), C], f"y{half}_{experts[0]}")
             cols = slice(half * P, (half + 1) * P)
             for j, e in enumerate(experts):
                 if e < HOT:
@@ -193,62 +187,63 @@ def tile_moe_hot_mlp_relu_kernel(
                 else:
                     w = late["w2c"][:, e - HOT, 2 * half * P:2 * (half + 1) * P].bitcast(FP4X4)
                     ws = s2c[:, e - HOT, cols]
-                mine = slice((e % 2) * C, (e % 2 + 1) * C)
                 nc.tensor.matmul_mx(out=acc[:, j, :], lhsT=w, lhsT_scale=ws,
-                                    rhs=hc[e // 2][:, mine].bitcast(FP8X4), rhs_scale=hs[e // 2][:, mine],
+                                    rhs=hc[e // 2][:, e % 2, :].bitcast(FP8X4), rhs_scale=hs[e // 2][:, e % 2, :],
                                     start=True, stop=True)
-            dst = y[half][:, experts[0] * C:(experts[-1] + 1) * C]
-            src = acc[:].rearrange("p j c -> p (j c)")
-            if engine == "s":
-                nc.scalar.copy(dst, src)
-            else:
-                nc.vector.tensor_copy(dst, src)
+            outs[experts[0], half] = acc
 
-        def late_load(e):
-            if e == 5:
-                late["w2h"] = kept([P, HOT, N], U32, "w2h", f"w1_{e}")
-                nc.sync.dma_start(out=late["w2h"][:].bitcast(I32),
-                                  in_=w2h_words.rearrange("e s p n d -> p (e s) (n d)").bitcast(I32))
-            elif e == 4:
-                late["w2c"] = kept([P, E - HOT, 2 * N], U8, "w2c", f"w1_{e}")
-                nc.sync.dma_start(out=late["w2c"][:].bitcast(I32),
-                                  in_=w2c_words.rearrange("e s p b -> p (e s) b").bitcast(I32))
-            elif e >= 6:
-                late[e - 6] = kept([P, 2, T], F32, f"gate{e}", f"w1_{e}")
-                nc.sync.dma_start(out=late[e - 6][:],
-                                  in_=gate[2 * (e - 6):2 * (e - 5)].rearrange("r p t -> p r t"))
+        def results(experts, half, copy):
+            copy(y[half][:, experts[0] * C:(experts[-1] + 1) * C],
+                 outs[experts[0], half][:].rearrange("p j c -> p (j c)"))
 
-        gather_scales(0)
-        gather_words(0, 2)
-        gather_words(1)
         for e in range(E):
-            layer1(e)
-            if e == 0:
-                gather_scales(1)
-            if HOT <= e + 3 < E:
-                gather_scales(e + 3)
-            if e + 2 < E:
-                gather_words(e + 2)
-            if e + 2 < HOT:
-                gather_scales(e + 2)
-            late_load(e)
-            if e == 2:
-                load_planes(s2h, w2h_scales)
-                load_planes(s2c, w2c_scales)
-                for r, pos in enumerate((pos1, pos2, pos3, pos4)):
-                    nc.sync.dma_start(pos_t[r][:], pos)
+            if e < HOT:
+                gather_scales(e)
+            if HOT <= e + 1 < E:
+                load_w1(e + 1)
+                gather_scales(e + 1)
+            gather_words(e)
+        late["w2h"] = kept([P, HOT, N], U32, "w2h")
+        nc.sync.dma_start(out=late["w2h"][:].bitcast(I32),
+                          in_=w2h_words.rearrange("e s p n d -> p (e s) (n d)").bitcast(I32))
+        load_planes(s2h, w2h_scales, nc.sync)
+        late["w2c"] = kept([P, E - HOT, 2 * N], U8, "w2c")
+        nc.sync.dma_start(out=late["w2c"][:].bitcast(I32),
+                          in_=w2c_words.rearrange("e s p b -> p (e s) b").bitcast(I32))
+        load_planes(s2c, w2c_scales, nc.sync)
+        for r, pos in enumerate((pos1, pos2, pos3, pos4)):
+            nc.sync.dma_start(pos_t[r][:], pos)
+        for g in range(2):
+            late[g] = kept([P, 2, T], F32, f"gate{g}")
+            nc.sync.dma_start(out=late[g][:], in_=gate[2 * g:2 * g + 2].rearrange("r p t -> p r t"))
+
+        for e in range(E):
+            for j in range(2):
+                layer1(e, j)
+                relu(e, j)
             if e >= 1:
                 turn(e - 1)
+                interleave(e - 1)
+        for pair in range(3):
+            quantise([2 * pair, 2 * pair + 1])
+        layer2([0, 1], 0, "d0")
         turn(E - 1)
-        for pair in range(4):
-            quantise(pair)
-        layer2([0, 1], 0, "s")
-        layer2([2, 3], 0, "v")
-        layer2([4, 5], 0, "s")
-        layer2([6], 0, "s")
-        layer2([7], 0, "v")
-        for pair in range(E // 2):
-            layer2([2 * pair, 2 * pair + 1], 1, "s")
+        results([0, 1], 0, nc.vector.tensor_copy)
+        interleave(E - 1, 0)
+        interleave(E - 1, 1)
+        layer2([2, 3], 0, "d1")
+        layer2([4, 5], 0, "r3")
+        results([2, 3], 0, nc.scalar.copy)
+        results([4, 5], 0, nc.scalar.copy)
+        quantise([6])
+        quantise([7])
+        layer2([6], 0, "r0")
+        layer2([7], 0, "r1")
+        results([6], 0, nc.vector.tensor_copy)
+        results([7], 0, nc.vector.tensor_copy)
+        for pair, tag in enumerate(("r2", "d0", "d1", "r3")):
+            layer2([2 * pair, 2 * pair + 1], 1, tag)
+            results([2 * pair, 2 * pair + 1], 1, nc.scalar.copy)
 
         prod = {}
 
@@ -257,27 +252,52 @@ def tile_moe_hot_mlp_relu_kernel(
             nc.vector.tensor_tensor(prod[half, r][:], y[half][:].indirect(pos_t[r][:]),
                                     late[r // 2][:, r % 2, :], MULT)
 
+        def add_turned(dst, half, r, c):
+            nc.tensor.matmul(dst, lhsT=prod[half, r][:, c * P:(c + 1) * P], rhs=ident[:],
+                             start=(r == 0), stop=(r == 2), is_transpose=True)
+
+        turned = [kept([P, 4, P], F32, f"turned{half}") for half in range(2)]
         part = {}
 
-        def add_three(half):
-            bank = ps_t.tile([P, 4, P], F32, name="bank")
-            for c in range(4):
-                for r in range(3):
-                    nc.tensor.matmul(bank[:, c, :], lhsT=prod[half, r][:, c * P:(c + 1) * P],
-                                     rhs=ident[:], start=(r == 0), stop=(r == 2), is_transpose=True)
-            turned = work.tile([P, 4, P], F32, name="turned")
-            nc.scalar.copy(turned[:], bank[:])
-            part[half] = ps_h.tile([P, T], F32, name="acc")
-            for c in range(4):
-                nc.tensor.transpose(part[half][:, c * P:(c + 1) * P], turned[:, c, :], ident[:])
+        def turn_back(half, c):
+            nc.tensor.transpose(part[half][:, c * P:(c + 1) * P], turned[half][:, c, :], ident[:])
 
-        for half in range(2):
+        for r in range(3):
+            fetch(0, r)
+        bank = bank_tile("c0", [P, 4, P], "three0")
+        for c in range(4):
             for r in range(3):
-                fetch(half, r)
-            add_three(half)
-        for half in range(2):
-            fetch(half, 3)
-        for half in range(2):
-            res = work.tile([P, T], F32, name="res")
-            nc.vector.tensor_tensor(res[:], part[half][:], prod[half, 3][:], ADD)
-            nc.sync.dma_start(out=out[half * P:(half + 1) * P, :], in_=res[:])
+                add_turned(bank[:, c, :], 0, r, c)
+        nc.scalar.copy(turned[0][:], bank[:])
+        banks = [bank_tile(tag, [P, P], f"three1_{tag}") for tag in ("r0", "r1", "r2", "r3")]
+        part[0] = bank_tile("c1", [P, T], "part0")
+        for r in range(3):
+            fetch(1, r)
+            for c in range(4):
+                add_turned(banks[c][:], 1, r, c)
+            if r == 0:
+                for c in range(4):
+                    turn_back(0, c)
+        part[1] = bank_tile("d0", [P, T], "part1")
+        for c in range(4):
+            nc.scalar.copy(turned[1][:, c, :], banks[c][:])
+            turn_back(1, c)
+
+        def fetch_last(cols):
+            last = kept([P, T // 2], F32, f"last{cols.start}")
+            nc.vector.tensor_tensor(last[:], y[1][:].indirect(pos_t[3][:, cols.start // 16:cols.stop // 16]),
+                                    late[1][:, 1, cols], MULT)
+            return last
+
+        def finish(half, cols, last):
+            res = kept([P, cols.stop - cols.start], F32, f"res{half}_{cols.start}")
+            nc.vector.tensor_tensor(res[:], part[half][:, cols], last[:], ADD)
+            nc.sync.dma_start(out=out[half * P:(half + 1) * P, cols], in_=res[:])
+
+        left, right = slice(0, T // 2), slice(T // 2, T)
+        fetch(0, 3)
+        last_left = fetch_last(left)
+        finish(0, slice(0, T), prod[0, 3])
+        last_right = fetch_last(right)
+        finish(1, left, last_left)
+        finish(1, right, last_right)

@@ -161,8 +161,10 @@ def tile_moe_hot_mlp_relu_kernel(
         def interleave(e, j=0):
             dst = hq[e // 2][:, e % 2, :].bitcast(F32).rearrange("p (j m u) -> p j m u", j=2, u=2)
             src = turned_h[e, j][:].rearrange("p j u m -> p j m u")
-            if e < E - 1:
+            if e < E - 3:
                 nc.scalar.copy(dst, src)
+            elif e < E - 1:
+                nc.vector.tensor_copy(dst, src)
             elif j == 0:
                 nc.scalar.copy(dst[:, 0:1], src)
             else:
@@ -223,25 +225,29 @@ def tile_moe_hot_mlp_relu_kernel(
                 relu(e, j)
             if e >= 1:
                 turn(e - 1)
+            if 1 <= e < E - 2:
                 interleave(e - 1)
-        for pair in range(3):
-            quantise([2 * pair, 2 * pair + 1])
-        layer2([0, 1], 0, "d0")
         turn(E - 1)
-        results([0, 1], 0, nc.vector.tensor_copy)
-        interleave(E - 1, 0)
-        interleave(E - 1, 1)
-        layer2([2, 3], 0, "d1")
-        layer2([4, 5], 0, "r3")
+        quantise([0, 1])
+        quantise([2, 3])
+        interleave(5)
+        quantise([4, 5])
+        interleave(6)
+        quantise([6])
+        layer2([0, 1], 0, "r0")
+        results([0, 1], 0, nc.scalar.copy)
+        interleave(7, 0)
+        interleave(7, 1)
+        quantise([7])
+        layer2([2, 3], 0, "r1")
+        layer2([4, 5], 0, "d0")
+        layer2([6], 0, "d1")
+        layer2([7], 0, "r3")
         results([2, 3], 0, nc.scalar.copy)
         results([4, 5], 0, nc.scalar.copy)
-        quantise([6])
-        quantise([7])
-        layer2([6], 0, "r0")
-        layer2([7], 0, "r1")
-        results([6], 0, nc.vector.tensor_copy)
+        results([6], 0, nc.scalar.copy)
         results([7], 0, nc.vector.tensor_copy)
-        for pair, tag in enumerate(("r2", "d0", "d1", "r3")):
+        for pair, tag in enumerate(("r3", "d1", "r3", "d1")):
             layer2([2 * pair, 2 * pair + 1], 1, tag)
             results([2 * pair, 2 * pair + 1], 1, nc.scalar.copy)
 
@@ -269,7 +275,7 @@ def tile_moe_hot_mlp_relu_kernel(
             for r in range(3):
                 add_turned(bank[:, c, :], 0, r, c)
         nc.scalar.copy(turned[0][:], bank[:])
-        banks = [bank_tile(tag, [P, P], f"three1_{tag}") for tag in ("r0", "r1", "r2", "r3")]
+        banks = [bank_tile(tag, [P, P], f"three1_{tag}") for tag in ("r0", "r1", "r2", "d0")]
         part[0] = bank_tile("c1", [P, T], "part0")
         for r in range(3):
             fetch(1, r)
@@ -278,7 +284,7 @@ def tile_moe_hot_mlp_relu_kernel(
             if r == 0:
                 for c in range(4):
                     turn_back(0, c)
-        part[1] = bank_tile("d0", [P, T], "part1")
+        part[1] = bank_tile("c0", [P, T], "part1")
         for c in range(4):
             nc.scalar.copy(turned[1][:, c, :], banks[c][:])
             turn_back(1, c)

@@ -155,13 +155,12 @@ def tile_moe_hot_mlp_relu_kernel(
                 turned_h[e, js[0]] = bank
 
         hq = [kept([P, 2, 4 * C], BF16, f"hq{pair}") for pair in range(E // 2)]
-        hc = [kept([P, 2, C], U32, f"hc{pair}") for pair in range(E // 2)]
-        hs = [kept([P, 2, C], U8, f"hs{pair}") for pair in range(E // 2)]
+        hc, hs = {}, {}
 
         def interleave(e, j=0):
             dst = hq[e // 2][:, e % 2, :].bitcast(F32).rearrange("p (j m u) -> p j m u", j=2, u=2)
             src = turned_h[e, j][:].rearrange("p j u m -> p j m u")
-            if e < E - 3:
+            if e < E - 2:
                 nc.scalar.copy(dst, src)
             elif e < E - 1:
                 nc.vector.tensor_copy(dst, src)
@@ -170,11 +169,14 @@ def tile_moe_hot_mlp_relu_kernel(
             else:
                 nc.vector.tensor_copy(dst[:, 1:2], src)
 
-        def quantise(experts):
-            pair, mine = experts[0] // 2, slice(experts[0] % 2, experts[-1] % 2 + 1)
-            nc.vector.quantize_mx(out=hc[pair][:, mine, :].rearrange("p a c -> p (a c)").bitcast(FP8X4),
-                                  scales=hs[pair][:, mine, :].rearrange("p a c -> p (a c)"),
-                                  in_=hq[pair][:, mine, :].rearrange("p a c -> p (a c)"))
+        def quantise(experts, tag=None):
+            first, count = experts[0], len(experts)
+            codes = kept([P, count * C], U32, f"hc{first}", tag)
+            scales = kept([P, count * C], U8, f"hs{first}")
+            values = hq[first // 2][:, first % 2:first % 2 + count, :].rearrange("p a c -> p (a c)")
+            nc.vector.quantize_mx(out=codes[:].bitcast(FP8X4), scales=scales[:], in_=values)
+            for j, e in enumerate(experts):
+                hc[e], hs[e] = codes[:, j * C:(j + 1) * C], scales[:, j * C:(j + 1) * C]
 
         late = {}
 
@@ -190,7 +192,7 @@ def tile_moe_hot_mlp_relu_kernel(
                     w = late["w2c"][:, e - HOT, 2 * half * P:2 * (half + 1) * P].bitcast(FP4X4)
                     ws = s2c[:, e - HOT, cols]
                 nc.tensor.matmul_mx(out=acc[:, j, :], lhsT=w, lhsT_scale=ws,
-                                    rhs=hc[e // 2][:, e % 2, :].bitcast(FP8X4), rhs_scale=hs[e // 2][:, e % 2, :],
+                                    rhs=hc[e].bitcast(FP8X4), rhs_scale=hs[e],
                                     start=True, stop=True)
             outs[experts[0], half] = acc
 
@@ -225,19 +227,18 @@ def tile_moe_hot_mlp_relu_kernel(
                 relu(e, j)
             if e >= 1:
                 turn(e - 1)
-            if 1 <= e < E - 2:
+            if 1 <= e < E - 1:
                 interleave(e - 1)
         turn(E - 1)
         quantise([0, 1])
         quantise([2, 3])
-        interleave(5)
         quantise([4, 5])
         interleave(6)
-        quantise([6])
         layer2([0, 1], 0, "r0")
         results([0, 1], 0, nc.scalar.copy)
         interleave(7, 0)
         interleave(7, 1)
+        quantise([6], "hb7_1")
         quantise([7])
         layer2([2, 3], 0, "r1")
         layer2([4, 5], 0, "d0")

@@ -6,6 +6,10 @@ from concourse.masks import make_identity
 K, T, E, C, H, N, HOT, TOP = 1024, 512, 8, 256, 512, 256, 4, 4
 S = E * C
 P = 128
+UNITS = S // P
+ORDER = (0, 1, 2, 4, 5, 6, 7, 3)
+XS_WIDTH = 768
+SLOTS = 7
 FLOPS = 2 * S * (K * H + H * N)
 
 F32 = mybir.dt.float32
@@ -37,17 +41,28 @@ def tile_moe_hot_mlp_relu_kernel(
         def kept(shape, dtype, name, tag=None):
             return keep.tile(shape, dtype, name=name, tag=tag or name, align_bytes=64)
 
+        def expert(place):
+            return ORDER[place]
+
+        def first_slot(unit):
+            return ORDER[unit // 2] * C + unit % 2 * P
+
+        def entries(unit, count):
+            return offs_t[:, first_slot(unit) // 16:(first_slot(unit) + count * P) // 16]
+
+        scale_groups = [(0, 4), (4, 2), (6, 2), (8, 2), (10, 2), (12, 2), (14, 2)]
+
         offs_t = lists.tile([P, S // 16], U16, name="offs_t")
         pos_t = [lists.tile([P, T // 16], U16, name=f"pos_t{r}") for r in range(TOP)]
-        xw = kept([P, 2, T], U32, "xw")
-        xs = kept([P, T], U8, "xs")
-        w1 = [kept([P, 2, H], U32, f"w1_{e}") if e < HOT else kept([P, 2, 2 * H], U8, f"w1_{e}")
-              for e in range(E)]
+        xw = kept([P, 2 * T], U32, "xw")
+        xs = kept([P, XS_WIDTH], U8, "xs")
+        w1h = [kept([P, 2, H], U32, f"w1h{e}") for e in range(HOT)]
+        w1c = [kept([P, 4, 2 * H], U8, f"w1c{g}") for g in range((E - HOT) // 2)]
         s1h = [kept([P, H], U8, f"s1h{g}") for g in range(HOT // 2)]
         s1c = kept([P, 2 * (E - HOT), H], U8, "s1c")
         s2h = kept([P, HOT, N], U8, "s2h")
         s2c = kept([P, E - HOT, N], U8, "s2c")
-        moved = kept([P, E - HOT, C], U8, "moved")
+        moved = kept([P, (E - HOT) * C], U8, "moved")
         ident0 = kept([P, P], F32, "ident0")
         ident = kept([P, P], F32, "ident")
 
@@ -57,10 +72,11 @@ def tile_moe_hot_mlp_relu_kernel(
         nc.vector.memset(xs[:].bitcast(I32), 0)
         nc.vector.memset(s1h[0][:].bitcast(I32), 0)
         nc.vector.memset(as_words(s1c), 0)
+        nc.vector.memset(moved[:].bitcast(I32), 0)
         nc.vector.memset(s1h[1][:].bitcast(I32), 0)
         make_identity(nc, ident0[:])
         nc.scalar.activation(ident[:], ident0[:], RELU)
-        for plane in (moved, s2h, s2c):
+        for plane in (s2h, s2c):
             nc.vector.memset(as_words(plane), 0)
 
         def load_planes(tile3, scales, queue):
@@ -69,199 +85,235 @@ def tile_moe_hot_mlp_relu_kernel(
             for r in range(4):
                 queue.dma_start(out=dst[r:P:32], in_=src[r])
 
-        def load_w1(e):
-            if e < HOT:
-                src = w1h_words[e].rearrange("s p i d -> p s (i d)")
-            else:
-                src = w1c_words[e - HOT].rearrange("s p b -> p s b")
-            nc.sync.dma_start(out=w1[e][:].bitcast(I32), in_=src.bitcast(I32))
+        def load_w1h(e):
+            nc.sync.dma_start(out=w1h[e][:].bitcast(I32),
+                              in_=w1h_words[e].rearrange("s p i d -> p s (i d)").bitcast(I32))
+
+        def load_w1c(g):
+            nc.sync.dma_start(out=w1c[g][:].bitcast(I32),
+                              in_=w1c_words[2 * g:2 * g + 2].rearrange("e s p b -> p (e s) b").bitcast(I32))
 
         s1h_src = w1h_scales.bitcast(I32).rearrange("(g a) s b n -> g (a s) b n", a=2)
 
-        def load_packed(g, queue):
+        def load_packed(g):
             for q in range(4):
-                queue.dma_start(out=s1h[g][:].bitcast(I32)[32 * q:32 * q + 16],
-                                in_=s1h_src[g, :, 4 * q:4 * q + 4, :])
+                nc.sync.dma_start(out=s1h[g][:].bitcast(I32)[32 * q:32 * q + 16],
+                                  in_=s1h_src[g, :, 4 * q:4 * q + 4, :])
 
-        nc.sync.dma_start(out=xw[:].bitcast(I32),
-                          in_=x_words.rearrange("s p t d -> p s (t d)").bitcast(I32))
-        for q in range(4):
-            nc.sync.dma_start(out=xs[:].bitcast(I32)[32 * q:32 * q + 8],
-                              in_=x_scales.bitcast(I32)[:, 4 * q:4 * q + 4, :])
+        def load_xw(s):
+            nc.sync.dma_start(out=xw[:, s * T:(s + 1) * T].bitcast(I32),
+                              in_=x_words[s].rearrange("p t d -> p (t d)").bitcast(I32))
+
+        def load_xs():
+            for q in range(4):
+                nc.sync.dma_start(out=xs[:, 0:T].bitcast(I32)[32 * q:32 * q + 8],
+                                  in_=x_scales.bitcast(I32)[:, 4 * q:4 * q + 4, :])
+
         nc.sync.dma_start(offs_t[:], offs)
-        load_w1(0)
-        load_packed(0, nc.sync)
-        load_w1(1)
-        load_w1(2)
-        load_packed(1, nc.sync)
-        load_w1(3)
+        load_xs()
+        load_xw(0)
+        load_xw(1)
+        load_w1h(0)
+        load_packed(0)
+        load_w1h(1)
+        load_w1h(2)
+        load_packed(1)
         load_planes(s1c, w1c_scales, nc.gpsimd)
 
-        gw, gs = {}, {}
+        ring = [(-1, f"slot{slot}") for slot in range(SLOTS)]
+        ring.extend((2 * place + 1, f"w1h{ORDER[place]}") for place in range(3))
+        slot_of = {}
 
-        def gather_words(e):
-            tiles = [kept([P, C], U32, f"gw{e}_{s}") for s in range(2)]
-            width = P if e == 0 else C
-            for first in range(0, C, width):
-                entries = offs_t[:, (e * C + first) // 16:(e * C + first + width) // 16]
-                for s in range(2):
-                    nc.vector.tensor_copy(tiles[s][:, first:first + width], xw[:, s, :].indirect(entries))
-            for s in range(2):
-                for j in range(2):
-                    gw[e, s, j] = tiles[s][:, j * P:(j + 1) * P]
+        def gathered(shape, dtype, name, last_unit):
+            taken = min(ring)
+            ring.remove(taken)
+            ring.append((last_unit, taken[1]))
+            slot_of[name] = taken[1]
+            return kept(shape, dtype, name, slot_of[name])
 
-        def gather_scales(e):
-            gs[e] = kept([P, C], U8, f"gs{e}")
-            nc.vector.tensor_copy(gs[e][:], xs[:].indirect(offs_t[:, e * C // 16:(e + 1) * C // 16]))
-            if e >= HOT:
-                nc.sync.dma_start(out=moved[:, e - HOT, :].bitcast(I32)[0:112],
-                                  in_=gs[e][:].bitcast(I32)[4:116])
+        gw, gs, gs_moved = {}, {}, {}
 
-        hb = {}
+        def gather_words(unit, count, s, wide=False):
+            tile = gathered([P, count * P], U32, f"gw{unit}_{s}", unit + count - 1)
+            window = xw[:] if wide else xw[:, s * T:(s + 1) * T]
+            nc.vector.tensor_copy(tile[:], window.indirect(entries(unit, count)))
+            for j in range(count):
+                gw[unit + j, s] = tile[:, j * P:(j + 1) * P]
+
+        def gather_scales(group):
+            unit, count = scale_groups[group]
+            tile = gathered([P, count * P], U8, f"gs{group}", unit + count - 1)
+            nc.vector.tensor_copy(tile[:], xs[:].indirect(entries(unit, count)))
+            for j in range(count):
+                gs[unit + j] = (tile, slice(j * P, (j + 1) * P))
+            cold = [u for u in range(unit, unit + count) if expert(u // 2) >= HOT]
+            if cold:
+                at = first_slot(cold[0]) - HOT * C
+                nc.sync.dma_start(out=moved[:, at:at + len(cold) * P].bitcast(I32)[0:112],
+                                  in_=tile[:, (cold[0] - unit) * P:(cold[-1] + 1 - unit) * P].bitcast(I32)[4:116])
+
+        gather_scales(0)
+        gather_words(0, 1, 0)
+        gather_words(1, 1, 0)
+        gather_words(0, 1, 1)
+        gather_words(1, 1, 1)
+        gather_words(2, 2, 0, wide=True)
+        gather_words(2, 2, 1)
+        load_w1c(0)
+        gather_scales(1)
+        for place in range(2, 6):
+            gather_scales(place)
+            if place == 3:
+                load_w1c(1)
+            gather_words(2 * place, 2, 0)
+            gather_words(2 * place, 2, 1)
+        load_w1h(3)
+        gather_words(12, 2, 0)
+        gather_words(12, 2, 1)
+        gather_scales(6)
+        for unit in (14, 15):
+            gather_words(unit, 1, 0)
+            gather_words(unit, 1, 1)
+
+        w2h = kept([P, HOT, N], U32, "w2h")
+        nc.sync.dma_start(out=w2h[:].bitcast(I32),
+                          in_=w2h_words.rearrange("e s p n d -> p (e s) (n d)").bitcast(I32))
+        load_planes(s2h, w2h_scales, nc.sync)
+        w2c = kept([P, E - HOT, 2 * N], U8, "w2c")
+        nc.sync.dma_start(out=w2c[:].bitcast(I32),
+                          in_=w2c_words.rearrange("e s p b -> p (e s) b").bitcast(I32))
+        load_planes(s2c, w2c_scales, nc.gpsimd)
+        for r, pos in enumerate((pos1, pos2, pos3, pos4)):
+            nc.sync.dma_start(pos_t[r][:], pos)
+        gates = kept([P, TOP, T], F32, "gates")
+        nc.sync.dma_start(out=gates[:], in_=gate.rearrange("r p t -> p r t"))
+
+        hb, sums, turned_h = {}, {}, {}
         y = [kept([P, S], F32, f"y{half}") for half in range(2)]
 
-        sums = {}
-
-        def layer1(e, j):
-            cols = slice(j * P, (j + 1) * P)
-            sums[e, j] = bank_tile(f"r{max(3 * e - 1 + j, j) % 4}", [P, H], f"sums{e}_{j}")
+        def layer1(unit):
+            e = expert(unit // 2)
+            sums[unit] = bank_tile(f"s{unit % 3}", [P, H], f"sums{unit}")
+            tile, cols = gs[unit]
             for s in range(2):
                 if e < HOT:
-                    w, ws = w1[e][:, s, :].bitcast(FP8X4), s1h[e // 2][4 * (2 * (e % 2) + s):P]
-                    ts = gs[e][4 * s:P, cols]
+                    w, ws = w1h[e][:, s, :].bitcast(FP8X4), s1h[e // 2][4 * (2 * (e % 2) + s):P]
+                    ts = tile[4 * s:P, cols]
                 else:
-                    w, ws = w1[e][:, s, :].bitcast(FP4X4), s1c[:, 2 * (e - HOT) + s, :]
-                    ts = gs[e][:, cols] if s == 0 else moved[:, e - HOT, cols]
-                nc.tensor.matmul_mx(out=sums[e, j][:], lhsT=gw[e, s, j].bitcast(FP8X4),
+                    w = w1c[(e - HOT) // 2][:, 2 * (e % 2) + s, :].bitcast(FP4X4)
+                    ws = s1c[:, 2 * (e - HOT) + s, :]
+                    at = first_slot(unit) - HOT * C
+                    ts = tile[:, cols] if s == 0 else moved[:, at:at + P]
+                nc.tensor.matmul_mx(out=sums[unit][:], lhsT=gw[unit, s].bitcast(FP8X4),
                                     lhsT_scale=ts, rhs=w, rhs_scale=ws,
                                     start=(s == 0), stop=(s == 1))
 
-        def relu(e, j):
-            hb[e, j] = kept([P, H], BF16, f"hb{e}_{j}")
-            dst = hb[e, j][:].rearrange("m (u p d) -> m u p d", u=2, d=2)
-            src = sums[e, j][:].rearrange("m (p u d) -> m u p d", u=2, d=2)
+        def relu(unit):
+            hb[unit] = kept([P, H], BF16, f"hb{unit}")
+            dst = hb[unit][:].rearrange("m (u p d) -> m u p d", u=2, d=2)
+            src = sums[unit][:].rearrange("m (p u d) -> m u p d", u=2, d=2)
             nc.scalar.activation(dst, src, RELU)
 
-        turned_h = {}
+        def turn_units(group):
+            return [2 * group, 2 * group + 1] if group < E - 1 else [UNITS - 2 + group - (E - 1)]
 
-        def turn(e):
-            groups = [(f"r{3 * e % 4}", (0, 1))] if e < E - 1 else [("c0", (0,)), ("c1", (1,))]
-            for tag, js in groups:
-                bank = bank_tile(tag, [P, len(js), 2, P], f"turned_h{e}_{js[0]}")
-                for i, j in enumerate(js):
-                    for u in range(2):
-                        nc.tensor.transpose(bank[:, i, u, :],
-                                            hb[e, j][:].bitcast(F32)[:, u * P:(u + 1) * P], ident[:])
-                turned_h[e, js[0]] = bank
+        def turn(group):
+            units = turn_units(group)
+            bank = bank_tile(f"t{group % 2}" if group < E else "c1", [P, len(units), 2, P], f"turned_h{group}")
+            for i, unit in enumerate(units):
+                for u in range(2):
+                    nc.tensor.transpose(bank[:, i, u, :],
+                                        hb[unit][:].bitcast(F32)[:, u * P:(u + 1) * P], ident[:])
+            turned_h[group] = bank
 
-        hq = [kept([P, 2, 4 * C], BF16, f"hq{pair}") for pair in range(E // 2)]
-        hc, hs = {}, {}
+        runs = [(0, 8), (8, 4), (12, 2), (14, 2)]
+        hq = [kept([P, count, H], BF16, f"hq{first}") for first, count in runs]
 
-        def interleave(e, j=0):
-            dst = hq[e // 2][:, e % 2, :].bitcast(F32).rearrange("p (j m u) -> p j m u", j=2, u=2)
-            src = turned_h[e, j][:].rearrange("p j u m -> p j m u")
-            if e < E - 2:
-                nc.scalar.copy(dst, src)
-            elif e < E - 1:
-                nc.vector.tensor_copy(dst, src)
-            elif j == 0:
-                nc.scalar.copy(dst[:, 0:1], src)
-            else:
-                nc.vector.tensor_copy(dst[:, 1:2], src)
+        def interleave(group, copy):
+            units = turn_units(group)
+            run = max(i for i, (first, count) in enumerate(runs) if first <= units[0])
+            at = units[0] - runs[run][0]
+            dst = hq[run][:, at:at + len(units), :].bitcast(F32).rearrange("p j (m u) -> p j m u", u=2)
+            copy(dst, turned_h[group][:].rearrange("p j u m -> p j m u"))
 
-        def quantise(experts, tag=None):
-            first, count = experts[0], len(experts)
-            codes = kept([P, count * C], U32, f"hc{first}", tag)
-            scales = kept([P, count * C], U8, f"hs{first}")
-            values = hq[first // 2][:, first % 2:first % 2 + count, :].rearrange("p a c -> p (a c)")
-            nc.vector.quantize_mx(out=codes[:].bitcast(FP8X4), scales=scales[:], in_=values)
-            for j, e in enumerate(experts):
-                hc[e], hs[e] = codes[:, j * C:(j + 1) * C], scales[:, j * C:(j + 1) * C]
+        for place in range(E):
+            for unit in (2 * place, 2 * place + 1):
+                layer1(unit)
+                relu(unit)
+            if place >= 1:
+                turn(place - 1)
+            if 1 <= place < E - 1:
+                interleave(place - 1, nc.scalar.copy)
+        for group in (E - 1, E):
+            turn(group)
+            interleave(group, nc.scalar.copy)
 
-        late = {}
+        codes = kept([P, S], U32, "codes", slot_of["gs5"])
+        scales = kept([P, S], U8, "scales")
+
+        def quantise(run):
+            first, count = runs[run]
+            cols = slice(first * P, (first + count) * P)
+            nc.vector.quantize_mx(out=codes[:, cols].bitcast(FP8X4), scales=scales[:, cols],
+                                  in_=hq[run][:].rearrange("p a c -> p (a c)"))
 
         outs = {}
 
-        def layer2(experts, half, tag):
-            acc = bank_tile(tag, [P, len(experts), C], f"y{half}_{experts[0]}")
+        def layer2(places, half, tag):
+            acc = bank_tile(tag, [P, len(places), C], f"y{half}_{places[0]}")
             cols = slice(half * P, (half + 1) * P)
-            for j, e in enumerate(experts):
+            for j, place in enumerate(places):
+                e = expert(place)
                 if e < HOT:
-                    w, ws = late["w2h"][:, e, cols].bitcast(FP8X4), s2h[:, e, cols]
+                    w, ws = w2h[:, e, cols].bitcast(FP8X4), s2h[:, e, cols]
                 else:
-                    w = late["w2c"][:, e - HOT, 2 * half * P:2 * (half + 1) * P].bitcast(FP4X4)
+                    w = w2c[:, e - HOT, 2 * half * P:2 * (half + 1) * P].bitcast(FP4X4)
                     ws = s2c[:, e - HOT, cols]
+                slots = slice(place * C, (place + 1) * C)
                 nc.tensor.matmul_mx(out=acc[:, j, :], lhsT=w, lhsT_scale=ws,
-                                    rhs=hc[e].bitcast(FP8X4), rhs_scale=hs[e],
+                                    rhs=codes[:, slots].bitcast(FP8X4), rhs_scale=scales[:, slots],
                                     start=True, stop=True)
-            outs[experts[0], half] = acc
+            outs[places[0], half] = acc
 
-        def results(experts, half, copy):
-            copy(y[half][:, experts[0] * C:(experts[-1] + 1) * C],
-                 outs[experts[0], half][:].rearrange("p j c -> p (j c)"))
+        def results(places, half, copy):
+            first, last = expert(places[0]), expert(places[-1])
+            by_expert = y[half][:].rearrange("p (e c) -> p e c", c=C)
+            copy(by_expert[:, first:last + 1:max(last - first, 1), :], outs[places[0], half][:])
 
-        for e in range(E):
-            if e < HOT:
-                gather_scales(e)
-            if HOT <= e + 1 < E:
-                load_w1(e + 1)
-                gather_scales(e + 1)
-            gather_words(e)
-        late["w2h"] = kept([P, HOT, N], U32, "w2h")
-        nc.sync.dma_start(out=late["w2h"][:].bitcast(I32),
-                          in_=w2h_words.rearrange("e s p n d -> p (e s) (n d)").bitcast(I32))
-        load_planes(s2h, w2h_scales, nc.sync)
-        late["w2c"] = kept([P, E - HOT, 2 * N], U8, "w2c")
-        nc.sync.dma_start(out=late["w2c"][:].bitcast(I32),
-                          in_=w2c_words.rearrange("e s p b -> p (e s) b").bitcast(I32))
-        load_planes(s2c, w2c_scales, nc.sync)
-        for r, pos in enumerate((pos1, pos2, pos3, pos4)):
-            nc.sync.dma_start(pos_t[r][:], pos)
-        for g in range(2):
-            late[g] = kept([P, 2, T], F32, f"gate{g}")
-            nc.sync.dma_start(out=late[g][:], in_=gate[2 * g:2 * g + 2].rearrange("r p t -> p r t"))
-
-        for e in range(E):
-            for j in range(2):
-                layer1(e, j)
-                relu(e, j)
-            if e >= 1:
-                turn(e - 1)
-            if 1 <= e < E - 1:
-                interleave(e - 1)
-        turn(E - 1)
-        quantise([0, 1])
-        quantise([2, 3])
-        quantise([4, 5])
-        interleave(6)
-        layer2([0, 1], 0, "r0")
+        quantise(0)
+        quantise(1)
+        interleave(E - 2, nc.vector.tensor_copy)
+        quantise(2)
+        quantise(3)
+        layer2([0, 1], 0, "s1")
         results([0, 1], 0, nc.scalar.copy)
-        interleave(7, 0)
-        interleave(7, 1)
-        quantise([6], "hb7_1")
-        quantise([7])
-        layer2([2, 3], 0, "r1")
-        layer2([4, 5], 0, "d0")
-        layer2([6], 0, "d1")
-        layer2([7], 0, "r3")
+        layer2([2, 3], 0, "s2")
         results([2, 3], 0, nc.scalar.copy)
-        results([4, 5], 0, nc.scalar.copy)
+        layer2([6], 0, "c0")
+        layer2([7], 0, "t0")
+        layer2([4, 5], 0, "c1")
+        results([4, 5], 0, nc.vector.tensor_copy)
         results([6], 0, nc.scalar.copy)
-        results([7], 0, nc.vector.tensor_copy)
-        for pair, tag in enumerate(("r3", "d1", "r3", "d1")):
-            layer2([2 * pair, 2 * pair + 1], 1, tag)
-            results([2 * pair, 2 * pair + 1], 1, nc.scalar.copy)
+        results([7], 0, nc.scalar.copy)
+        for pair, tag in enumerate(("c0", "c1", "c0", "c1")):
+            places = [ORDER.index(2 * pair), ORDER.index(2 * pair + 1)]
+            layer2(places, 1, tag)
+            results(places, 1, nc.scalar.copy)
 
-        prod = {}
 
-        def fetch(half, r):
-            prod[half, r] = kept([P, T], F32, f"prod{half}_{r}")
-            nc.vector.tensor_tensor(prod[half, r][:], y[half][:].indirect(pos_t[r][:]),
-                                    late[r // 2][:, r % 2, :], MULT)
+        prods = {}
 
-        def add_turned(dst, half, r, c):
-            nc.tensor.matmul(dst, lhsT=prod[half, r][:, c * P:(c + 1) * P], rhs=ident[:],
-                             start=(r == 0), stop=(r == 2), is_transpose=True)
+        def fetch(half, r, cols):
+            product = kept([P, cols.stop - cols.start], F32, f"prod{half}_{r}_{cols.start}")
+            prods[half, r, cols.start] = product
+            nc.vector.tensor_tensor(product[:],
+                                    y[half][:].indirect(pos_t[r][:, cols.start // 16:cols.stop // 16]),
+                                    gates[:, r, cols], MULT)
+            return product
+
+        def add_turned(dst, product, r, c):
+            nc.tensor.matmul(dst, lhsT=product[:, c * P:(c + 1) * P], rhs=ident[:],
+                             start=(r == 0), stop=(r == TOP - 2), is_transpose=True)
 
         turned = [kept([P, 4, P], F32, f"turned{half}") for half in range(2)]
         part = {}
@@ -269,32 +321,26 @@ def tile_moe_hot_mlp_relu_kernel(
         def turn_back(half, c):
             nc.tensor.transpose(part[half][:, c * P:(c + 1) * P], turned[half][:, c, :], ident[:])
 
-        for r in range(3):
-            fetch(0, r)
-        bank = bank_tile("c0", [P, 4, P], "three0")
+        whole = slice(0, T)
+        products = [fetch(0, r, whole) for r in range(TOP - 1)]
+        bank = bank_tile("c2", [P, 4, P], "three0")
         for c in range(4):
-            for r in range(3):
-                add_turned(bank[:, c, :], 0, r, c)
+            for r in range(TOP - 1):
+                add_turned(bank[:, c, :], products[r], r, c)
         nc.scalar.copy(turned[0][:], bank[:])
-        banks = [bank_tile(tag, [P, P], f"three1_{tag}") for tag in ("r0", "r1", "r2", "d0")]
+        banks = [bank_tile(tag, [P, P], f"three1_{tag}") for tag in ("s0", "s1", "s2", "t1")]
         part[0] = bank_tile("c1", [P, T], "part0")
-        for r in range(3):
-            fetch(1, r)
+        for r in range(TOP - 1):
+            product = fetch(1, r, whole)
             for c in range(4):
-                add_turned(banks[c][:], 1, r, c)
+                add_turned(banks[c][:], product, r, c)
             if r == 0:
                 for c in range(4):
                     turn_back(0, c)
-        part[1] = bank_tile("c0", [P, T], "part1")
+        part[1] = bank_tile("c2", [P, T], "part1")
         for c in range(4):
             nc.scalar.copy(turned[1][:, c, :], banks[c][:])
             turn_back(1, c)
-
-        def fetch_last(cols):
-            last = kept([P, T // 2], F32, f"last{cols.start}")
-            nc.vector.tensor_tensor(last[:], y[1][:].indirect(pos_t[3][:, cols.start // 16:cols.stop // 16]),
-                                    late[1][:, 1, cols], MULT)
-            return last
 
         def finish(half, cols, last):
             res = kept([P, cols.stop - cols.start], F32, f"res{half}_{cols.start}")
@@ -302,9 +348,9 @@ def tile_moe_hot_mlp_relu_kernel(
             nc.sync.dma_start(out=out[half * P:(half + 1) * P, cols], in_=res[:])
 
         left, right = slice(0, T // 2), slice(T // 2, T)
-        fetch(0, 3)
-        last_left = fetch_last(left)
-        finish(0, slice(0, T), prod[0, 3])
-        last_right = fetch_last(right)
+        last_whole = fetch(0, TOP - 1, whole)
+        last_left = fetch(1, TOP - 1, left)
+        finish(0, whole, last_whole)
+        last_right = fetch(1, TOP - 1, right)
         finish(1, left, last_left)
         finish(1, right, last_right)

@@ -9,6 +9,7 @@ P = 128
 UNITS = S // P
 ORDER = (0, 1, 2, 4, 5, 6, 7, 3)
 XS_WIDTH = 768
+HELD = {1: "c0", 2: "c2"}
 SLOTS = 7
 FLOPS = 2 * S * (K * H + H * N)
 
@@ -56,7 +57,7 @@ def tile_moe_hot_mlp_relu_kernel(
         pos_t = [lists.tile([P, T // 16], U16, name=f"pos_t{r}") for r in range(TOP)]
         xw = kept([P, 2 * T], U32, "xw")
         xs = kept([P, XS_WIDTH], U8, "xs")
-        w1h = [kept([P, 2, H], U32, f"w1h{e}") for e in range(HOT)]
+        w1h = [kept([P, 2, H], U32, f"w1h{e}") for e in range(HOT - 1)]
         w1c = [kept([P, 4, 2 * H], U8, f"w1c{g}") for g in range((E - HOT) // 2)]
         s1h = [kept([P, H], U8, f"s1h{g}") for g in range(HOT // 2)]
         s1c = kept([P, 2 * (E - HOT), H], U8, "s1c")
@@ -71,10 +72,10 @@ def tile_moe_hot_mlp_relu_kernel(
 
         nc.vector.memset(xs[:].bitcast(I32), 0)
         nc.vector.memset(s1h[0][:].bitcast(I32), 0)
-        nc.vector.memset(as_words(s1c), 0)
         nc.vector.memset(moved[:].bitcast(I32), 0)
         nc.vector.memset(s1h[1][:].bitcast(I32), 0)
         make_identity(nc, ident0[:])
+        nc.gpsimd.memset(as_words(s1c), 0)
         nc.scalar.activation(ident[:], ident0[:], RELU)
         for plane in (s2h, s2c):
             nc.vector.memset(as_words(plane), 0)
@@ -86,6 +87,8 @@ def tile_moe_hot_mlp_relu_kernel(
                 queue.dma_start(out=dst[r:P:32], in_=src[r])
 
         def load_w1h(e):
+            if e == HOT - 1:
+                w1h.append(kept([P, 2, H], U32, f"w1h{e}", "w1h1"))
             nc.sync.dma_start(out=w1h[e][:].bitcast(I32),
                               in_=w1h_words[e].rearrange("s p i d -> p s (i d)").bitcast(I32))
 
@@ -109,9 +112,9 @@ def tile_moe_hot_mlp_relu_kernel(
                 nc.sync.dma_start(out=xs[:, 0:T].bitcast(I32)[32 * q:32 * q + 8],
                                   in_=x_scales.bitcast(I32)[:, 4 * q:4 * q + 4, :])
 
+        load_xw(0)
         nc.sync.dma_start(offs_t[:], offs)
         load_xs()
-        load_xw(0)
         load_xw(1)
         load_w1h(0)
         load_packed(0)
@@ -121,7 +124,7 @@ def tile_moe_hot_mlp_relu_kernel(
         load_planes(s1c, w1c_scales, nc.gpsimd)
 
         ring = [(-1, f"slot{slot}") for slot in range(SLOTS)]
-        ring.extend((2 * place + 1, f"w1h{ORDER[place]}") for place in range(3))
+        ring.extend((2 * place + 1, f"w1h{ORDER[place]}") for place in range(1))
         slot_of = {}
 
         def gathered(shape, dtype, name, last_unit):
@@ -152,9 +155,9 @@ def tile_moe_hot_mlp_relu_kernel(
                 nc.sync.dma_start(out=moved[:, at:at + len(cold) * P].bitcast(I32)[0:112],
                                   in_=tile[:, (cold[0] - unit) * P:(cold[-1] + 1 - unit) * P].bitcast(I32)[4:116])
 
-        gather_scales(0)
         gather_words(0, 1, 0)
         gather_words(1, 1, 0)
+        gather_scales(0)
         gather_words(0, 1, 1)
         gather_words(1, 1, 1)
         gather_words(2, 2, 0, wide=True)
@@ -175,7 +178,7 @@ def tile_moe_hot_mlp_relu_kernel(
             gather_words(unit, 1, 0)
             gather_words(unit, 1, 1)
 
-        w2h = kept([P, HOT, N], U32, "w2h")
+        w2h = kept([P, HOT, N], U32, "w2h", "w1h2")
         nc.sync.dma_start(out=w2h[:].bitcast(I32),
                           in_=w2h_words.rearrange("e s p n d -> p (e s) (n d)").bitcast(I32))
         load_planes(s2h, w2h_scales, nc.sync)
@@ -185,7 +188,7 @@ def tile_moe_hot_mlp_relu_kernel(
         load_planes(s2c, w2c_scales, nc.gpsimd)
         for r, pos in enumerate((pos1, pos2, pos3, pos4)):
             nc.sync.dma_start(pos_t[r][:], pos)
-        gates = kept([P, TOP, T], F32, "gates")
+        gates = kept([P, TOP, T], F32, "gates", "w1c0")
         nc.sync.dma_start(out=gates[:], in_=gate.rearrange("r p t -> p r t"))
 
         hb, sums, turned_h = {}, {}, {}
@@ -193,7 +196,8 @@ def tile_moe_hot_mlp_relu_kernel(
 
         def layer1(unit):
             e = expert(unit // 2)
-            sums[unit] = bank_tile(f"s{unit % 3}", [P, H], f"sums{unit}")
+            tag = HELD.get(unit // 2 - 1) if unit % 2 == 0 else None
+            sums[unit] = bank_tile(tag or f"s{unit % 3}", [P, H], f"sums{unit}")
             tile, cols = gs[unit]
             for s in range(2):
                 if e < HOT:
@@ -219,7 +223,11 @@ def tile_moe_hot_mlp_relu_kernel(
 
         def turn(group):
             units = turn_units(group)
-            bank = bank_tile(f"t{group % 2}" if group < E else "c1", [P, len(units), 2, P], f"turned_h{group}")
+            if group in HELD:
+                tag = HELD[group]
+            else:
+                tag = f"t{group % 2}" if group < E else "c1"
+            bank = bank_tile(tag, [P, len(units), 2, P], f"turned_h{group}")
             for i, unit in enumerate(units):
                 for u in range(2):
                     nc.tensor.transpose(bank[:, i, u, :],

@@ -57,7 +57,7 @@ def tile_moe_hot_mlp_relu_kernel(
         pos_t = [lists.tile([P, T // 16], U16, name=f"pos_t{r}") for r in range(TOP)]
         xw = kept([P, 2 * T], U32, "xw")
         xs = kept([P, XS_WIDTH], U8, "xs")
-        w1h = [kept([P, 2, H], U32, f"w1h{e}") for e in range(HOT - 1)]
+        w1h = [kept([P, 2, H], U32, f"w1h{e}") for e in range(HOT)]
         w1c = [kept([P, 4, 2 * H], U8, f"w1c{g}") for g in range((E - HOT) // 2)]
         s1h = [kept([P, H], U8, f"s1h{g}") for g in range(HOT // 2)]
         s1c = kept([P, 2 * (E - HOT), H], U8, "s1c")
@@ -72,10 +72,10 @@ def tile_moe_hot_mlp_relu_kernel(
 
         nc.vector.memset(xs[:].bitcast(I32), 0)
         nc.vector.memset(s1h[0][:].bitcast(I32), 0)
+        nc.vector.memset(as_words(s1c), 0)
         nc.vector.memset(moved[:].bitcast(I32), 0)
         nc.vector.memset(s1h[1][:].bitcast(I32), 0)
         make_identity(nc, ident0[:])
-        nc.gpsimd.memset(as_words(s1c), 0)
         nc.scalar.activation(ident[:], ident0[:], RELU)
         for plane in (s2h, s2c):
             nc.vector.memset(as_words(plane), 0)
@@ -87,8 +87,6 @@ def tile_moe_hot_mlp_relu_kernel(
                 queue.dma_start(out=dst[r:P:32], in_=src[r])
 
         def load_w1h(e):
-            if e == HOT - 1:
-                w1h.append(kept([P, 2, H], U32, f"w1h{e}", "w1h1"))
             nc.sync.dma_start(out=w1h[e][:].bitcast(I32),
                               in_=w1h_words[e].rearrange("s p i d -> p s (i d)").bitcast(I32))
 
@@ -124,7 +122,7 @@ def tile_moe_hot_mlp_relu_kernel(
         load_planes(s1c, w1c_scales, nc.gpsimd)
 
         ring = [(-1, f"slot{slot}") for slot in range(SLOTS)]
-        ring.extend((2 * place + 1, f"w1h{ORDER[place]}") for place in range(1))
+        ring.extend((2 * place + 1, f"w1h{ORDER[place]}") for place in range(3))
         slot_of = {}
 
         def gathered(shape, dtype, name, last_unit):
@@ -134,7 +132,7 @@ def tile_moe_hot_mlp_relu_kernel(
             slot_of[name] = taken[1]
             return kept(shape, dtype, name, slot_of[name])
 
-        gw, gs, gs_moved = {}, {}, {}
+        gw, gs = {}, {}
 
         def gather_words(unit, count, s, wide=False):
             tile = gathered([P, count * P], U32, f"gw{unit}_{s}", unit + count - 1)
@@ -178,7 +176,7 @@ def tile_moe_hot_mlp_relu_kernel(
             gather_words(unit, 1, 0)
             gather_words(unit, 1, 1)
 
-        w2h = kept([P, HOT, N], U32, "w2h", "w1h2")
+        w2h = kept([P, HOT, N], U32, "w2h")
         nc.sync.dma_start(out=w2h[:].bitcast(I32),
                           in_=w2h_words.rearrange("e s p n d -> p (e s) (n d)").bitcast(I32))
         load_planes(s2h, w2h_scales, nc.sync)
@@ -188,7 +186,7 @@ def tile_moe_hot_mlp_relu_kernel(
         load_planes(s2c, w2c_scales, nc.gpsimd)
         for r, pos in enumerate((pos1, pos2, pos3, pos4)):
             nc.sync.dma_start(pos_t[r][:], pos)
-        gates = kept([P, TOP, T], F32, "gates", "w1c0")
+        gates = kept([P, TOP, T], F32, "gates")
         nc.sync.dma_start(out=gates[:], in_=gate.rearrange("r p t -> p r t"))
 
         hb, sums, turned_h = {}, {}, {}
@@ -250,7 +248,7 @@ def tile_moe_hot_mlp_relu_kernel(
                 relu(unit)
             if place >= 1:
                 turn(place - 1)
-            if 1 <= place < E - 1:
+            if 1 <= place <= 7:
                 interleave(place - 1, nc.scalar.copy)
         for group in (E - 1, E):
             turn(group)
@@ -288,21 +286,18 @@ def tile_moe_hot_mlp_relu_kernel(
             by_expert = y[half][:].rearrange("p (e c) -> p e c", c=C)
             copy(by_expert[:, first:last + 1:max(last - first, 1), :], outs[places[0], half][:])
 
-        quantise(0)
-        quantise(1)
-        interleave(E - 2, nc.vector.tensor_copy)
-        quantise(2)
-        quantise(3)
+        for run in range(len(runs)):
+            quantise(run)
         layer2([0, 1], 0, "s1")
         results([0, 1], 0, nc.scalar.copy)
         layer2([2, 3], 0, "s2")
         results([2, 3], 0, nc.scalar.copy)
+        layer2([4, 5], 0, "s0")
+        results([4, 5], 0, nc.scalar.copy)
         layer2([6], 0, "c0")
-        layer2([7], 0, "t0")
-        layer2([4, 5], 0, "c1")
-        results([4, 5], 0, nc.vector.tensor_copy)
+        layer2([7], 0, "c1")
         results([6], 0, nc.scalar.copy)
-        results([7], 0, nc.scalar.copy)
+        results([7], 0, nc.vector.tensor_copy)
         for pair, tag in enumerate(("c0", "c1", "c0", "c1")):
             places = [ORDER.index(2 * pair), ORDER.index(2 * pair + 1)]
             layer2(places, 1, tag)

@@ -7,7 +7,7 @@ K, T, E, C, H, N, HOT, TOP = 1024, 512, 8, 256, 512, 256, 4, 4
 S = E * C
 P = 128
 UNITS = S // P
-ORDER = (0, 1, 2, 4, 5, 6, 7, 3)
+ORDER = (0, 1, 3, 4, 5, 6, 7, 2)
 XS_WIDTH = 768
 HELD = {1: "c0", 2: "c2"}
 SLOTS = 7
@@ -117,7 +117,7 @@ def tile_moe_hot_mlp_relu_kernel(
         load_w1h(0)
         load_packed(0)
         load_w1h(1)
-        load_w1h(2)
+        load_w1h(ORDER[2])
         load_packed(1)
         load_planes(s1c, w1c_scales, nc.gpsimd)
 
@@ -166,9 +166,9 @@ def tile_moe_hot_mlp_relu_kernel(
             gather_scales(place)
             if place == 3:
                 load_w1c(1)
+                load_w1h(ORDER[-1])
             gather_words(2 * place, 2, 0)
             gather_words(2 * place, 2, 1)
-        load_w1h(3)
         gather_words(12, 2, 0)
         gather_words(12, 2, 1)
         gather_scales(6)
@@ -188,6 +188,15 @@ def tile_moe_hot_mlp_relu_kernel(
             nc.sync.dma_start(pos_t[r][:], pos)
         gates = kept([P, TOP, T], F32, "gates")
         nc.sync.dma_start(out=gates[:], in_=gate.rearrange("r p t -> p r t"))
+
+        last = ORDER[-1]
+        w1p = kept([P, 2, H], U32, "w1p")
+        s1p = kept([P, H], U8, "s1p")
+        nc.gpsimd.tensor_copy(s1p[:].rearrange("p (t a b) -> p a t b", t=4, b=16),
+                              s1h[last // 2][:].rearrange("p (a b t) -> p a t b", t=4, b=16))
+        for s in range(2):
+            nc.gpsimd.tensor_copy(w1p[:, s, :].rearrange("p (t a b) -> p a t b", t=4, b=4),
+                                  w1h[last][:, s, :].rearrange("p (a b t) -> p a t b", t=4, b=4))
 
         hb, sums, turned_h = {}, {}, {}
         y = [kept([P, S], F32, f"y{half}") for half in range(2)]
@@ -217,14 +226,14 @@ def tile_moe_hot_mlp_relu_kernel(
             nc.scalar.activation(dst, src, RELU)
 
         def turn_units(group):
-            return [2 * group, 2 * group + 1] if group < E - 1 else [UNITS - 2 + group - (E - 1)]
+            return [2 * group, 2 * group + 1]
 
         def turn(group):
             units = turn_units(group)
             if group in HELD:
                 tag = HELD[group]
             else:
-                tag = f"t{group % 2}" if group < E else "c1"
+                tag = f"t{group % 2}"
             bank = bank_tile(tag, [P, len(units), 2, P], f"turned_h{group}")
             for i, unit in enumerate(units):
                 for u in range(2):
@@ -232,7 +241,7 @@ def tile_moe_hot_mlp_relu_kernel(
                                         hb[unit][:].bitcast(F32)[:, u * P:(u + 1) * P], ident[:])
             turned_h[group] = bank
 
-        runs = [(0, 8), (8, 4), (12, 2), (14, 2)]
+        runs = [(0, 8), (8, 4), (12, 2), (14, 1), (15, 1)]
         hq = [kept([P, count, H], BF16, f"hq{first}") for first, count in runs]
 
         def interleave(group, copy):
@@ -242,17 +251,30 @@ def tile_moe_hot_mlp_relu_kernel(
             dst = hq[run][:, at:at + len(units), :].bitcast(F32).rearrange("p j (m u) -> p j m u", u=2)
             copy(dst, turned_h[group][:].rearrange("p j u m -> p j m u"))
 
-        for place in range(E):
+        def layer1_direct(unit):
+            acc = bank_tile(f"s{unit % 3}", [P, 4, P], f"sums{unit}")
+            tile, cols = gs[unit]
+            for s in range(2):
+                for t in range(4):
+                    rows = slice(t * P, (t + 1) * P)
+                    nc.tensor.matmul_mx(out=acc[:, t, :], lhsT=w1p[:, s, rows].bitcast(FP8X4),
+                                        lhsT_scale=s1p[4 * s:P, rows],
+                                        rhs=gw[unit, s].bitcast(FP8X4), rhs_scale=tile[4 * s:P, cols],
+                                        start=(s == 0 and t == 0), stop=(s == 1 and t == 3))
+            dst = hq[unit - UNITS + len(runs)][:, 0, :].rearrange("p (m t) -> p m t", t=4)
+            nc.scalar.activation(dst, acc[:].rearrange("p t m -> p m t"), RELU)
+
+        for place in range(E - 1):
             for unit in (2 * place, 2 * place + 1):
                 layer1(unit)
                 relu(unit)
             if place >= 1:
                 turn(place - 1)
-            if 1 <= place <= 7:
                 interleave(place - 1, nc.scalar.copy)
-        for group in (E - 1, E):
-            turn(group)
-            interleave(group, nc.scalar.copy)
+        layer1_direct(UNITS - 2)
+        turn(E - 2)
+        interleave(E - 2, nc.scalar.copy)
+        layer1_direct(UNITS - 1)
 
         codes = kept([P, S], U32, "codes", slot_of["gs5"])
         scales = kept([P, S], U8, "scales")
@@ -295,8 +317,8 @@ def tile_moe_hot_mlp_relu_kernel(
         layer2([4, 5], 0, "s0")
         results([4, 5], 0, nc.scalar.copy)
         layer2([6], 0, "c0")
+        results([6], 0, nc.vector.tensor_copy)
         layer2([7], 0, "c1")
-        results([6], 0, nc.scalar.copy)
         results([7], 0, nc.vector.tensor_copy)
         for pair, tag in enumerate(("c0", "c1", "c0", "c1")):
             places = [ORDER.index(2 * pair), ORDER.index(2 * pair + 1)]

@@ -336,46 +336,44 @@ def tile_moe_hot_mlp_relu_kernel(
                                     gates[:, r, cols], MULT)
             return product
 
-        def add_turned(dst, product, r, c):
-            nc.tensor.matmul(dst, lhsT=product[:, c * P:(c + 1) * P], rhs=ident[:],
-                             start=(r == 0), stop=(r == TOP - 2), is_transpose=True)
-
-        turned = [kept([P, 4, P], F32, f"turned{half}") for half in range(2)]
-        part = {}
-
-        def turn_back(half, c):
-            nc.tensor.transpose(part[half][:, c * P:(c + 1) * P], turned[half][:, c, :], ident[:])
-
         whole = slice(0, T)
-        products = [fetch(0, r, whole) for r in range(TOP - 1)]
-        bank = bank_tile("c2", [P, 4, P], "three0")
-        for c in range(4):
-            for r in range(TOP - 1):
-                add_turned(bank[:, c, :], products[r], r, c)
-        nc.scalar.copy(turned[0][:], bank[:])
-        banks = [bank_tile(tag, [P, P], f"three1_{tag}") for tag in ("s0", "s1", "s2", "t1")]
-        part[0] = bank_tile("c1", [P, T], "part0")
-        for r in range(TOP - 1):
-            product = fetch(1, r, whole)
-            for c in range(4):
-                add_turned(banks[c][:], product, r, c)
-            if r == 0:
-                for c in range(4):
-                    turn_back(0, c)
-        part[1] = bank_tile("c2", [P, T], "part1")
-        for c in range(4):
-            nc.scalar.copy(turned[1][:, c, :], banks[c][:])
-            turn_back(1, c)
+        sides = (slice(0, T // 2), slice(T // 2, T))
+        turned = [kept([P, 4, P], F32, f"turned{half}") for half in range(2)]
 
-        def finish(half, cols, last):
-            res = kept([P, cols.stop - cols.start], F32, f"res{half}_{cols.start}")
-            nc.vector.tensor_tensor(res[:], part[half][:, cols], last[:], ADD)
-            nc.sync.dma_start(out=out[half * P:(half + 1) * P, cols], in_=res[:])
+        def sum_banks(half):
+            return [bank_tile(tag, [P, P], f"sum{half}_{tag}") for tag in ("s0", "s1", "s2", "t1")]
 
-        left, right = slice(0, T // 2), slice(T // 2, T)
-        last_whole = fetch(0, TOP - 1, whole)
-        last_left = fetch(1, TOP - 1, left)
-        finish(0, whole, last_whole)
-        last_right = fetch(1, TOP - 1, right)
-        finish(1, left, last_left)
-        finish(1, right, last_right)
+        def add_turned(banks, half, r, cols, count):
+            product = fetch(half, r, cols)
+            for c in range(cols.start // P, cols.stop // P):
+                at = c * P - cols.start
+                nc.tensor.matmul(banks[c][:], lhsT=product[:, at:at + P], rhs=ident[:],
+                                 start=(r == 0), stop=(r == count - 1), is_transpose=True)
+
+        def turn_back(banks, half, cols, tag):
+            blocks = range(cols.start // P, cols.stop // P)
+            back = bank_tile(tag, [P, len(blocks), P], f"back{half}_{cols.start}")
+            for i, c in enumerate(blocks):
+                nc.scalar.copy(turned[half][:, c, :], banks[c][:])
+                nc.tensor.transpose(back[:, i, :], turned[half][:, c, :], ident[:])
+            return back[:].rearrange("p a b -> p (a b)")
+
+        banks = sum_banks(0)
+        for r in range(TOP):
+            add_turned(banks, 0, r, whole, TOP)
+        res = kept([P, T], F32, "res0")
+        nc.scalar.copy(res[:], turn_back(banks, 0, whole, "c2"))
+        nc.sync.dma_start(out=out[0:P, :], in_=res[:])
+
+        banks = sum_banks(1)
+        for r in range(TOP - 2):
+            add_turned(banks, 1, r, whole, TOP - 1)
+        back = []
+        for cols, tag in zip(sides, ("t0", "c0")):
+            add_turned(banks, 1, TOP - 2, cols, TOP - 1)
+            back.append(turn_back(banks, 1, cols, tag))
+        last = [fetch(1, TOP - 1, cols) for cols in sides]
+        for side, cols in enumerate(sides):
+            res = kept([P, T // 2], F32, f"res1_{side}")
+            nc.vector.tensor_tensor(res[:], back[side], last[side][:], ADD)
+            nc.sync.dma_start(out=out[P:2 * P, cols], in_=res[:])

@@ -161,12 +161,12 @@ def tile_moe_hot_mlp_relu_kernel(
         gather_words(2, 2, 0, wide=True)
         gather_words(2, 2, 1)
         load_w1c(0)
-        gather_scales(1)
+        gather_scales(2)
         for place in range(2, 6):
-            gather_scales(place)
+            gather_scales(1 if place == 2 else place)
             if place == 3:
-                load_w1c(1)
                 load_w1h(ORDER[-1])
+                load_w1c(1)
             gather_words(2 * place, 2, 0)
             gather_words(2 * place, 2, 1)
         gather_words(12, 2, 0)

@@ -57,7 +57,7 @@ def tile_moe_hot_mlp_relu_kernel(
         pos_t = [lists.tile([P, T // 16], U16, name=f"pos_t{r}") for r in range(TOP)]
         xw = kept([P, 2 * T], U32, "xw")
         xs = kept([P, XS_WIDTH], U8, "xs")
-        w1h = [kept([P, 2, H], U32, f"w1h{e}") for e in range(HOT)]
+        w1h = {e: kept([P, 2, H], U32, f"w1h{e}") for e in ORDER[:3]}
         w1c = [kept([P, 4, 2 * H], U8, f"w1c{g}") for g in range((E - HOT) // 2)]
         s1h = [kept([P, H], U8, f"s1h{g}") for g in range(HOT // 2)]
         s1c = kept([P, 2 * (E - HOT), H], U8, "s1c")
@@ -86,8 +86,8 @@ def tile_moe_hot_mlp_relu_kernel(
             for r in range(4):
                 queue.dma_start(out=dst[r:P:32], in_=src[r])
 
-        def load_w1h(e):
-            nc.sync.dma_start(out=w1h[e][:].bitcast(I32),
+        def load_w1h(e, queue=nc.sync):
+            queue.dma_start(out=w1h[e][:].bitcast(I32),
                               in_=w1h_words[e].rearrange("s p i d -> p s (i d)").bitcast(I32))
 
         def load_w1c(g):
@@ -120,6 +120,8 @@ def tile_moe_hot_mlp_relu_kernel(
         load_w1h(ORDER[2])
         load_packed(1)
         load_planes(s1c, w1c_scales, nc.gpsimd)
+        w1h[ORDER[-1]] = kept([P, 2, H], U32, "w1h_last", "ident0")
+        load_w1h(ORDER[-1], nc.gpsimd)
 
         ring = [(-1, f"slot{slot}") for slot in range(SLOTS)]
         ring.extend((2 * place + 1, f"w1h{ORDER[place]}") for place in range(3))
@@ -165,7 +167,6 @@ def tile_moe_hot_mlp_relu_kernel(
         for place in range(2, 6):
             gather_scales(1 if place == 2 else place)
             if place == 3:
-                load_w1h(ORDER[-1])
                 load_w1c(1)
             gather_words(2 * place, 2, 0)
             gather_words(2 * place, 2, 1)

@@ -155,15 +155,17 @@ def tile_moe_hot_mlp_relu_kernel(
                 nc.sync.dma_start(out=moved[:, at:at + len(cold) * P].bitcast(I32)[0:112],
                                   in_=tile[:, (cold[0] - unit) * P:(cold[-1] + 1 - unit) * P].bitcast(I32)[4:116])
 
-        gather_words(0, 1, 0)
+        first_words = kept([P, P], U32, "first_words")
+        nc.vector.tensor_copy(first_words[:], xw[:, 0:T].indirect(entries(0, 1)))
+        gw[0, 0] = first_words[:]
         gather_words(1, 1, 0)
         gather_scales(0)
+        load_w1c(0)
+        gather_scales(2)
         gather_words(0, 1, 1)
         gather_words(1, 1, 1)
         gather_words(2, 2, 0, wide=True)
         gather_words(2, 2, 1)
-        load_w1c(0)
-        gather_scales(2)
         for place in range(2, 6):
             gather_scales(1 if place == 2 else place)
             if place == 3:

@@ -7,6 +7,7 @@ K, T, E, C, H, N, HOT, TOP = 1024, 512, 8, 256, 512, 256, 4, 4
 S = E * C
 P = 128
 UNITS = S // P
+BLOCKS = T // P
 ORDER = (0, 1, 3, 4, 5, 6, 7, 2)
 XS_WIDTH = 768
 HELD = {1: "c0", 2: "c2"}
@@ -22,6 +23,7 @@ U8 = mybir.dt.uint8
 FP8X4 = mybir.dt.float8_e4m3fn_x4
 FP4X4 = mybir.dt.float4_e2m1fn_x4
 RELU = mybir.ActivationFunctionType.Relu
+COPY = mybir.ActivationFunctionType.Copy
 MULT = mybir.AluOpType.mult
 ADD = mybir.AluOpType.add
 
@@ -187,10 +189,16 @@ def tile_moe_hot_mlp_relu_kernel(
         nc.sync.dma_start(out=w2c[:].bitcast(I32),
                           in_=w2c_words.rearrange("e s p b -> p (e s) b").bitcast(I32))
         load_planes(s2c, w2c_scales, nc.gpsimd)
-        for r, pos in enumerate((pos1, pos2, pos3, pos4)):
-            nc.sync.dma_start(pos_t[r][:], pos)
         gates = kept([P, TOP, T], F32, "gates")
         nc.sync.dma_start(out=gates[:], in_=gate.rearrange("r p t -> p r t"))
+        for r, pos in enumerate((pos1, pos2, pos3, pos4)):
+            nc.sync.dma_start(pos_t[r][:], pos)
+        gcol = kept([P, TOP - 1, BLOCKS], F32, "gcol")
+        with nc.allow_non_contiguous_dma(reason="one gate value a partition"):
+            runs_of_gate = gate.rearrange("r q (c p) -> (r q c) p", p=P)
+            step = P + 1
+            nc.sync.dma_start(out=gcol[:].rearrange("p r c -> p (r c)"),
+                              in_=runs_of_gate[0:(TOP - 1) * BLOCKS * step:step].rearrange("j p -> p j"))
 
         last = ORDER[-1]
         w1p = kept([P, 2, H], U32, "w1p")
@@ -328,55 +336,54 @@ def tile_moe_hot_mlp_relu_kernel(
             layer2(places, 1, tag)
             results(places, 1, nc.scalar.copy)
 
-
-        prods = {}
-
-        def fetch(half, r, cols):
-            product = kept([P, cols.stop - cols.start], F32, f"prod{half}_{r}_{cols.start}")
-            prods[half, r, cols.start] = product
-            nc.vector.tensor_tensor(product[:],
-                                    y[half][:].indirect(pos_t[r][:, cols.start // 16:cols.stop // 16]),
-                                    gates[:, r, cols], MULT)
+        def fused(half, r):
+            product = kept([P, T], F32, f"prod{half}_{r}")
+            nc.vector.tensor_tensor(product[:], y[half][:].indirect(pos_t[r][:]), gates[:, r, :], MULT)
             return product
 
-        whole = slice(0, T)
-        sides = (slice(0, T // 2), slice(T // 2, T))
-        turned = [kept([P, 4, P], F32, f"turned{half}") for half in range(2)]
+        def plain(half, r):
+            picked = kept([P, T], F32, f"pick{half}_{r}")
+            nc.scalar.activation(picked[:], y[half][:].indirect(pos_t[r][:]), COPY)
+            return picked
 
-        def sum_banks(half):
-            return [bank_tile(tag, [P, P], f"sum{half}_{tag}") for tag in ("s0", "s1", "s2", "t1")]
+        def turn_into(acc, src, first, last):
+            for c in range(BLOCKS):
+                cols = slice(c * P, (c + 1) * P)
+                nc.tensor.matmul(acc[:, cols], lhsT=src[:, cols], rhs=ident[:], is_transpose=True,
+                                 start=(first and c == 0), stop=(last and c == BLOCKS - 1))
 
-        def add_turned(banks, half, r, cols, count):
-            product = fetch(half, r, cols)
-            for c in range(cols.start // P, cols.stop // P):
-                at = c * P - cols.start
-                nc.tensor.matmul(banks[c][:], lhsT=product[:, at:at + P], rhs=ident[:],
-                                 start=(r == 0), stop=(r == count - 1), is_transpose=True)
+        def scale_on_vector(src, r):
+            scaled = kept([P, BLOCKS, P], F32, f"scaled{r}")
+            nc.vector.tensor_tensor(scaled[:], src[:].rearrange("p (c n) -> p c n", n=P),
+                                    gcol[:, r, :].unsqueeze(2).to_broadcast([P, BLOCKS, P]), MULT)
+            return scaled[:].rearrange("p c n -> p (c n)")
 
-        def turn_back(banks, half, cols, tag):
-            blocks = range(cols.start // P, cols.stop // P)
-            back = bank_tile(tag, [P, len(blocks), P], f"back{half}_{cols.start}")
-            for i, c in enumerate(blocks):
-                nc.scalar.copy(turned[half][:, c, :], banks[c][:])
-                nc.tensor.transpose(back[:, i, :], turned[half][:, c, :], ident[:])
-            return back[:].rearrange("p a b -> p (a b)")
+        def scale_on_scalar(src, r):
+            scaled = kept([P, T], F32, f"scaled{r}")
+            for c in range(BLOCKS):
+                cols = slice(c * P, (c + 1) * P)
+                nc.scalar.activation(scaled[:, cols], src[:, cols], COPY, scale=gcol[:, r, c:c + 1])
+            return scaled[:]
 
-        banks = sum_banks(0)
-        for r in range(TOP):
-            add_turned(banks, 0, r, whole, TOP)
-        res = kept([P, T], F32, "res0")
-        nc.scalar.copy(res[:], turn_back(banks, 0, whole, "c2"))
-        nc.sync.dma_start(out=out[0:P, :], in_=res[:])
-
-        banks = sum_banks(1)
-        for r in range(TOP - 2):
-            add_turned(banks, 1, r, whole, TOP - 1)
-        back = []
-        for cols, tag in zip(sides, ("t0", "c0")):
-            add_turned(banks, 1, TOP - 2, cols, TOP - 1)
-            back.append(turn_back(banks, 1, cols, tag))
-        last = [fetch(1, TOP - 1, cols) for cols in sides]
-        for side, cols in enumerate(sides):
-            res = kept([P, T // 2], F32, f"res1_{side}")
-            nc.vector.tensor_tensor(res[:], back[side], last[side][:], ADD)
-            nc.sync.dma_start(out=out[P:2 * P, cols], in_=res[:])
+        products = [fused(0, r) for r in range(TOP)]
+        rest = fused(1, TOP - 1)
+        picked = [plain(1, r) for r in range(TOP - 1)]
+        sum0 = bank_tile("c1", [P, T], "sum0")
+        by_token = [bank_tile(tag, [P, T], f"by_token{r}") for r, tag in enumerate(("s0", "s1", "s2"))]
+        turn_into(sum0, products[0], True, False)
+        turn_into(sum0, products[1], False, False)
+        turn_into(by_token[0], picked[0], True, True)
+        turn_into(sum0, products[2], False, True)
+        turn_into(by_token[1], picked[1], True, True)
+        turn_into(by_token[2], picked[2], True, True)
+        sum0_sb = kept([P, T], F32, "sum0_sb")
+        nc.scalar.copy(sum0_sb[:], sum0[:])
+        back = [bank_tile(tag, [P, T], f"back{half}") for half, tag in enumerate(("t0", "t1"))]
+        turn_into(back[1], scale_on_vector(by_token[0], 0), True, False)
+        turn_into(back[0], sum0_sb[:], True, True)
+        turn_into(back[1], scale_on_vector(by_token[1], 1), False, False)
+        turn_into(back[1], scale_on_scalar(by_token[2], 2), False, True)
+        for half, other in enumerate((products[TOP - 1], rest)):
+            res = kept([P, T], F32, f"res{half}")
+            nc.vector.tensor_tensor(res[:], back[half][:], other[:], ADD)
+            nc.sync.dma_start(out=out[half * P:(half + 1) * P, :], in_=res[:])

@@ -189,16 +189,10 @@ def tile_moe_hot_mlp_relu_kernel(
         nc.sync.dma_start(out=w2c[:].bitcast(I32),
                           in_=w2c_words.rearrange("e s p b -> p (e s) b").bitcast(I32))
         load_planes(s2c, w2c_scales, nc.gpsimd)
-        gates = kept([P, TOP, T], F32, "gates")
-        nc.sync.dma_start(out=gates[:], in_=gate.rearrange("r p t -> p r t"))
         for r, pos in enumerate((pos1, pos2, pos3, pos4)):
             nc.sync.dma_start(pos_t[r][:], pos)
-        gcol = kept([P, TOP - 1, BLOCKS], F32, "gcol")
-        with nc.allow_non_contiguous_dma(reason="one gate value a partition"):
-            runs_of_gate = gate.rearrange("r q (c p) -> (r q c) p", p=P)
-            step = P + 1
-            nc.sync.dma_start(out=gcol[:].rearrange("p r c -> p (r c)"),
-                              in_=runs_of_gate[0:(TOP - 1) * BLOCKS * step:step].rearrange("j p -> p j"))
+        gates = kept([P, TOP, T], F32, "gates")
+        nc.sync.dma_start(out=gates[:], in_=gate.rearrange("r p t -> p r t"))
 
         last = ORDER[-1]
         w1p = kept([P, 2, H], U32, "w1p")
@@ -331,59 +325,62 @@ def tile_moe_hot_mlp_relu_kernel(
         results([6], 0, nc.vector.tensor_copy)
         layer2([7], 0, "c1")
         results([7], 0, nc.vector.tensor_copy)
-        for pair, tag in enumerate(("c0", "c1", "c0", "c1")):
-            places = [ORDER.index(2 * pair), ORDER.index(2 * pair + 1)]
-            layer2(places, 1, tag)
-            results(places, 1, nc.scalar.copy)
 
-        def fused(half, r):
-            product = kept([P, T], F32, f"prod{half}_{r}")
-            nc.vector.tensor_tensor(product[:], y[half][:].indirect(pos_t[r][:]), gates[:, r, :], MULT)
+        def fused(half, r, cols=slice(0, T)):
+            product = kept([P, cols.stop - cols.start], F32, f"prod{half}_{r}_{cols.start}")
+            nc.vector.tensor_tensor(product[:], y[half][:].indirect(pos_t[r][:, cols.start // 16:cols.stop // 16]),
+                                    gates[:, r, cols], MULT)
             return product
 
-        def plain(half, r):
-            picked = kept([P, T], F32, f"pick{half}_{r}")
+        def plain(half, r, tag=None):
+            picked = kept([P, T], F32, f"pick{half}_{r}", tag)
             nc.scalar.activation(picked[:], y[half][:].indirect(pos_t[r][:]), COPY)
             return picked
 
         def turn_into(acc, src, first, last):
-            for c in range(BLOCKS):
+            blocks = src.shape[1] // P
+            for c in range(blocks):
                 cols = slice(c * P, (c + 1) * P)
                 nc.tensor.matmul(acc[:, cols], lhsT=src[:, cols], rhs=ident[:], is_transpose=True,
-                                 start=(first and c == 0), stop=(last and c == BLOCKS - 1))
+                                 start=(first and c == 0), stop=(last and c == blocks - 1))
 
-        def scale_on_vector(src, r):
-            scaled = kept([P, BLOCKS, P], F32, f"scaled{r}")
-            nc.vector.tensor_tensor(scaled[:], src[:].rearrange("p (c n) -> p c n", n=P),
-                                    gcol[:, r, :].unsqueeze(2).to_broadcast([P, BLOCKS, P]), MULT)
-            return scaled[:].rearrange("p c n -> p (c n)")
+        picked0 = plain(0, 0)
+        for pair, tag in ((0, "s1"), (2, "s2"), (3, "s0"), (1, "c1")):
+            places = [ORDER.index(2 * pair), ORDER.index(2 * pair + 1)]
+            layer2(places, 1, tag)
+            results(places, 1, nc.scalar.copy)
 
-        def scale_on_scalar(src, r):
-            scaled = kept([P, T], F32, f"scaled{r}")
-            for c in range(BLOCKS):
-                cols = slice(c * P, (c + 1) * P)
-                nc.scalar.activation(scaled[:, cols], src[:, cols], COPY, scale=gcol[:, r, c:c + 1])
-            return scaled[:]
+        def gated(picked, half, r):
+            product = kept([P, T], F32, f"prod{half}_{r}")
+            nc.vector.tensor_tensor(product[:], picked[:], gates[:, r, :], MULT)
+            return product
 
-        products = [fused(0, r) for r in range(TOP)]
-        rest = fused(1, TOP - 1)
-        picked = [plain(1, r) for r in range(TOP - 1)]
-        sum0 = bank_tile("c1", [P, T], "sum0")
-        by_token = [bank_tile(tag, [P, T], f"by_token{r}") for r, tag in enumerate(("s0", "s1", "s2"))]
-        turn_into(sum0, products[0], True, False)
-        turn_into(sum0, products[1], False, False)
-        turn_into(by_token[0], picked[0], True, True)
-        turn_into(sum0, products[2], False, True)
-        turn_into(by_token[1], picked[1], True, True)
-        turn_into(by_token[2], picked[2], True, True)
+        picked1 = plain(1, TOP - 1)
+        sum0 = bank_tile("c2", [P, T], "sum0")[:]
+        for r in range(1, TOP):
+            turn_into(sum0, fused(0, r)[:], r == 1, False)
+        turn_into(sum0, gated(picked0, 0, 0)[:], False, True)
         sum0_sb = kept([P, T], F32, "sum0_sb")
-        nc.scalar.copy(sum0_sb[:], sum0[:])
-        back = [bank_tile(tag, [P, T], f"back{half}") for half, tag in enumerate(("t0", "t1"))]
-        turn_into(back[1], scale_on_vector(by_token[0], 0), True, False)
-        turn_into(back[0], sum0_sb[:], True, True)
-        turn_into(back[1], scale_on_vector(by_token[1], 1), False, False)
-        turn_into(back[1], scale_on_scalar(by_token[2], 2), False, True)
-        for half, other in enumerate((products[TOP - 1], rest)):
-            res = kept([P, T], F32, f"res{half}")
-            nc.vector.tensor_tensor(res[:], back[half][:], other[:], ADD)
-            nc.sync.dma_start(out=out[half * P:(half + 1) * P, :], in_=res[:])
+        nc.scalar.copy(sum0_sb[:], sum0)
+
+        sides = (slice(0, T // 2), slice(T // 2, T))
+        sum1 = [bank_tile(tag, [P, T // 2], f"sum1_{tag}")[:] for tag in ("s0", "s1")]
+        for first, product in ((True, fused(1, 0)), (False, gated(picked1, 1, TOP - 1))):
+            for side, cols in enumerate(sides):
+                turn_into(sum1[side], product[:, cols], first, False)
+        back0 = bank_tile("s2", [P, T], "back0")[:]
+        turn_into(back0, sum0_sb[:], True, True)
+        back1 = [bank_tile(tag, [P, T // 2], f"back1_{tag}")[:] for tag in ("t0", "t1")]
+        for side, cols in enumerate(sides):
+            turn_into(sum1[side], fused(1, 1, cols)[:], False, True)
+            sum1_sb = kept([P, T // 2], F32, f"sum1_sb{side}")
+            nc.scalar.copy(sum1_sb[:], sum1[side])
+            turn_into(back1[side], sum1_sb[:], True, True)
+        rest = [fused(1, 2, cols) for cols in sides]
+        res0 = kept([P, T], F32, "res0")
+        nc.scalar.copy(res0[:], back0)
+        nc.sync.dma_start(out=out[0:P, :], in_=res0[:])
+        for side, cols in enumerate(sides):
+            res = kept([P, T // 2], F32, f"res1_{side}")
+            nc.vector.tensor_tensor(res[:], back1[side], rest[side][:], ADD)
+            nc.sync.dma_start(out=out[P:2 * P, cols], in_=res[:])

@@ -344,43 +344,47 @@ def tile_moe_hot_mlp_relu_kernel(
                 nc.tensor.matmul(acc[:, cols], lhsT=src[:, cols], rhs=ident[:], is_transpose=True,
                                  start=(first and c == 0), stop=(last and c == blocks - 1))
 
-        picked0 = plain(0, 0)
         for pair, tag in ((0, "s1"), (2, "s2"), (3, "s0"), (1, "c1")):
             places = [ORDER.index(2 * pair), ORDER.index(2 * pair + 1)]
             layer2(places, 1, tag)
             results(places, 1, nc.scalar.copy)
 
-        def gated(picked, half, r):
-            product = kept([P, T], F32, f"prod{half}_{r}")
-            nc.vector.tensor_tensor(product[:], picked[:], gates[:, r, :], MULT)
+        def gated(picked, half, r, cols=slice(0, T)):
+            product = kept([P, cols.stop - cols.start], F32, f"prod{half}_{r}_{cols.start}")
+            nc.vector.tensor_tensor(product[:], picked[:, cols], gates[:, r, cols], MULT)
             return product
 
-        picked1 = plain(1, TOP - 1)
+        picked0 = plain(0, 0)
         sum0 = bank_tile("c2", [P, T], "sum0")[:]
         for r in range(1, TOP):
-            turn_into(sum0, fused(0, r)[:], r == 1, False)
-        turn_into(sum0, gated(picked0, 0, 0)[:], False, True)
+            turn_into(sum0, fused(0, r)[:], r == 1, r == TOP - 1)
         sum0_sb = kept([P, T], F32, "sum0_sb")
         nc.scalar.copy(sum0_sb[:], sum0)
+        picked1 = plain(1, TOP - 1, "prod0_3_0")
+        back0 = bank_tile("s2", [P, T], "back0")[:]
+        turn_into(back0, sum0_sb[:], True, True)
 
         sides = (slice(0, T // 2), slice(T // 2, T))
         sum1 = [bank_tile(tag, [P, T // 2], f"sum1_{tag}")[:] for tag in ("s0", "s1")]
-        for first, product in ((True, fused(1, 0)), (False, gated(picked1, 1, TOP - 1))):
-            for side, cols in enumerate(sides):
-                turn_into(sum1[side], product[:, cols], first, False)
-        back0 = bank_tile("s2", [P, T], "back0")[:]
-        turn_into(back0, sum0_sb[:], True, True)
         back1 = [bank_tile(tag, [P, T // 2], f"back1_{tag}")[:] for tag in ("t0", "t1")]
+        for r in range(2):
+            product = fused(1, r)
+            for side, cols in enumerate(sides):
+                turn_into(sum1[side], product[:, cols], r == 0, False)
+        rest0 = gated(picked0, 0, 0)
+        res0 = kept([P, T], F32, "res0")
+        nc.vector.tensor_tensor(res0[:], back0, rest0[:], ADD)
+        nc.sync.dma_start(out=out[0:P, :], in_=res0[:])
         for side, cols in enumerate(sides):
-            turn_into(sum1[side], fused(1, 1, cols)[:], False, True)
+            turn_into(sum1[side], gated(picked1, 1, TOP - 1, cols)[:], False, True)
             sum1_sb = kept([P, T // 2], F32, f"sum1_sb{side}")
             nc.scalar.copy(sum1_sb[:], sum1[side])
             turn_into(back1[side], sum1_sb[:], True, True)
-        rest = [fused(1, 2, cols) for cols in sides]
-        res0 = kept([P, T], F32, "res0")
-        nc.scalar.copy(res0[:], back0)
-        nc.sync.dma_start(out=out[0:P, :], in_=res0[:])
+        rest = kept([P, T], F32, "rest", "prod0_3_0")
+        for cols in sides:
+            nc.vector.tensor_tensor(rest[:, cols], y[1][:].indirect(pos_t[2][:, cols.start // 16:cols.stop // 16]),
+                                    gates[:, 2, cols], MULT)
         for side, cols in enumerate(sides):
             res = kept([P, T // 2], F32, f"res1_{side}")
-            nc.vector.tensor_tensor(res[:], back1[side], rest[side][:], ADD)
+            nc.vector.tensor_tensor(res[:], back1[side], rest[:, cols], ADD)
             nc.sync.dma_start(out=out[P:2 * P, cols], in_=res[:])

@@ -371,9 +371,10 @@ def tile_moe_hot_mlp_relu_kernel(
             product = fused(1, r)
             for side, cols in enumerate(sides):
                 turn_into(sum1[side], product[:, cols], r == 0, False)
-        rest0 = gated(picked0, 0, 0)
+        rest0 = [gated(picked0, 0, 0, cols) for cols in sides]
         res0 = kept([P, T], F32, "res0")
-        nc.vector.tensor_tensor(res0[:], back0, rest0[:], ADD)
+        for side, cols in enumerate(sides):
+            nc.vector.tensor_tensor(res0[:, cols], back0[:, cols], rest0[side][:], ADD)
         nc.sync.dma_start(out=out[0:P, :], in_=res0[:])
         for side, cols in enumerate(sides):
             turn_into(sum1[side], gated(picked1, 1, TOP - 1, cols)[:], False, True)

@@ -332,9 +332,9 @@ def tile_moe_hot_mlp_relu_kernel(
                                     gates[:, r, cols], MULT)
             return product
 
-        def plain(half, r, tag=None):
-            picked = kept([P, T], F32, f"pick{half}_{r}", tag)
-            nc.scalar.activation(picked[:], y[half][:].indirect(pos_t[r][:]), COPY)
+        def plain(half, r, tag=None, cols=slice(0, T)):
+            picked = kept([P, cols.stop - cols.start], F32, f"pick{half}_{r}", tag)
+            nc.scalar.activation(picked[:], y[half][:].indirect(pos_t[r][:, cols.start // 16:cols.stop // 16]), COPY)
             return picked
 
         def turn_into(acc, src, first, last):
@@ -365,6 +365,7 @@ def tile_moe_hot_mlp_relu_kernel(
         turn_into(back0, sum0_sb[:], True, True)
 
         sides = (slice(0, T // 2), slice(T // 2, T))
+        picked2 = plain(1, TOP - 2, "sum0_sb", sides[1])
         sum1 = [bank_tile(tag, [P, T // 2], f"sum1_{tag}")[:] for tag in ("s0", "s1")]
         back1 = [bank_tile(tag, [P, T // 2], f"back1_{tag}")[:] for tag in ("t0", "t1")]
         for r in range(2):
@@ -382,9 +383,8 @@ def tile_moe_hot_mlp_relu_kernel(
             nc.scalar.copy(sum1_sb[:], sum1[side])
             turn_into(back1[side], sum1_sb[:], True, True)
         rest = kept([P, T], F32, "rest", "prod0_3_0")
-        for cols in sides:
-            nc.vector.tensor_tensor(rest[:, cols], y[1][:].indirect(pos_t[2][:, cols.start // 16:cols.stop // 16]),
-                                    gates[:, 2, cols], MULT)
+        nc.vector.tensor_tensor(rest[:, sides[0]], y[1][:].indirect(pos_t[2][:, 0:T // 32]), gates[:, 2, sides[0]], MULT)
+        nc.vector.tensor_tensor(rest[:, sides[1]], picked2[:], gates[:, 2, sides[1]], MULT)
         for side, cols in enumerate(sides):
             res = kept([P, T // 2], F32, f"res1_{side}")
             nc.vector.tensor_tensor(res[:], back1[side], rest[:, cols], ADD)

@@ -333,7 +333,7 @@ def tile_moe_hot_mlp_relu_kernel(
             return product
 
         def plain(half, r, tag=None, cols=slice(0, T)):
-            picked = kept([P, cols.stop - cols.start], F32, f"pick{half}_{r}", tag)
+            picked = kept([P, cols.stop - cols.start], F32, f"pick{half}_{r}_{cols.start}", tag)
             nc.scalar.activation(picked[:], y[half][:].indirect(pos_t[r][:, cols.start // 16:cols.stop // 16]), COPY)
             return picked
 
@@ -354,38 +354,57 @@ def tile_moe_hot_mlp_relu_kernel(
             nc.vector.tensor_tensor(product[:], picked[:, cols], gates[:, r, cols], MULT)
             return product
 
-        picked0 = plain(0, 0)
-        sum0 = bank_tile("c2", [P, T], "sum0")[:]
-        for r in range(1, TOP):
-            turn_into(sum0, fused(0, r)[:], r == 1, r == TOP - 1)
-        sum0_sb = kept([P, T], F32, "sum0_sb")
-        nc.scalar.copy(sum0_sb[:], sum0)
-        picked1 = plain(1, TOP - 1, "prod0_3_0")
-        back0 = bank_tile("s2", [P, T], "back0")[:]
-        turn_into(back0, sum0_sb[:], True, True)
+        def warm_up(tag, passes):
+            idle = bank_tile(tag, [P, H], f"warm_{tag}")
+            for i in range(passes):
+                nc.tensor.matmul_mx(out=idle[:], lhsT=w2h[:, 0, 0:P].bitcast(FP8X4), lhsT_scale=s2h[:, 0, 0:P],
+                                    rhs=codes[:, 0:H].bitcast(FP8X4), rhs_scale=scales[:, 0:H],
+                                    start=(i == 0), stop=(i == passes - 1))
 
         sides = (slice(0, T // 2), slice(T // 2, T))
-        picked2 = plain(1, TOP - 2, "sum0_sb", sides[1])
-        sum1 = [bank_tile(tag, [P, T // 2], f"sum1_{tag}")[:] for tag in ("s0", "s1")]
-        back1 = [bank_tile(tag, [P, T // 2], f"back1_{tag}")[:] for tag in ("t0", "t1")]
-        for r in range(2):
-            product = fused(1, r)
+        warm_up("s0", 1)
+        warm_up("c1", 1)
+        picked0 = plain(0, 0)
+        picked1 = [plain(1, TOP - 1, None, sides[0])]
+        sum0 = [bank_tile(tag, [P, T // 2], f"sum0_{tag}")[:] for tag in ("c2", "c0")]
+        for r in range(1, TOP - 1):
+            product = fused(0, r)
             for side, cols in enumerate(sides):
-                turn_into(sum1[side], product[:, cols], r == 0, False)
-        rest0 = [gated(picked0, 0, 0, cols) for cols in sides]
-        res0 = kept([P, T], F32, "res0")
+                turn_into(sum0[side], product[:, cols], r == 1, False)
         for side, cols in enumerate(sides):
-            nc.vector.tensor_tensor(res0[:, cols], back0[:, cols], rest0[side][:], ADD)
-        nc.sync.dma_start(out=out[0:P, :], in_=res0[:])
+            turn_into(sum0[side], fused(0, TOP - 1, cols)[:], False, True)
+        sum0_sb = kept([P, T], F32, "sum0_sb")
         for side, cols in enumerate(sides):
-            turn_into(sum1[side], gated(picked1, 1, TOP - 1, cols)[:], False, True)
+            nc.scalar.copy(sum0_sb[:, cols], sum0[side])
+        picked1.append(plain(1, TOP - 1, "prod0_3_0", sides[1]))
+        picked2 = plain(1, TOP - 2, f"prod0_3_{T // 2}")
+        warm_up("c2", 2)
+        back0 = bank_tile("s2", [P, T], "back0")[:]
+        sum1 = [bank_tile(tag, [P, T // 2], f"sum1_{tag}")[:] for tag in ("c2", "s1")]
+        back1 = [bank_tile(tag, [P, T // 2], f"back1_{tag}")[:] for tag in ("t0", "t1")]
+
+        product = fused(1, 0)
+        for side, cols in enumerate(sides):
+            turn_into(sum1[side], product[:, cols], True, False)
+        turn_into(back0, sum0_sb[:], True, True)
+        for side, cols in enumerate(sides):
+            product = kept([P, T // 2], F32, f"prod1_3_{side}")
+            nc.vector.tensor_tensor(product[:], picked1[side][:], gates[:, TOP - 1, cols], MULT)
+            turn_into(sum1[side], product[:], False, False)
+            turn_into(sum1[side], fused(1, 1, cols)[:], False, True)
+        for side in range(2):
             sum1_sb = kept([P, T // 2], F32, f"sum1_sb{side}")
             nc.scalar.copy(sum1_sb[:], sum1[side])
             turn_into(back1[side], sum1_sb[:], True, True)
-        rest = kept([P, T], F32, "rest", "prod0_3_0")
-        nc.vector.tensor_tensor(rest[:, sides[0]], y[1][:].indirect(pos_t[2][:, 0:T // 32]), gates[:, 2, sides[0]], MULT)
-        nc.vector.tensor_tensor(rest[:, sides[1]], picked2[:], gates[:, 2, sides[1]], MULT)
+        rest0 = kept([P, T], F32, "rest0", "prod0_3_0")
+        for cols in sides:
+            nc.vector.tensor_tensor(rest0[:, cols], picked0[:, cols], gates[:, 0, cols], MULT)
+        res0 = kept([P, T], F32, "res0")
+        for side, cols in enumerate(sides):
+            nc.vector.tensor_tensor(res0[:, cols], back0[:, cols], rest0[:, cols], ADD)
+        nc.sync.dma_start(out=out[0:P, :], in_=res0[:])
+        rest1 = [gated(picked2, 1, TOP - 2, cols) for cols in sides]
         for side, cols in enumerate(sides):
             res = kept([P, T // 2], F32, f"res1_{side}")
-            nc.vector.tensor_tensor(res[:], back1[side], rest[:, cols], ADD)
+            nc.vector.tensor_tensor(res[:], back1[side], rest1[side][:], ADD)
             nc.sync.dma_start(out=out[P:2 * P, cols], in_=res[:])

@@ -354,16 +354,7 @@ def tile_moe_hot_mlp_relu_kernel(
             nc.vector.tensor_tensor(product[:], picked[:, cols], gates[:, r, cols], MULT)
             return product
 
-        def warm_up(tag, passes):
-            idle = bank_tile(tag, [P, H], f"warm_{tag}")
-            for i in range(passes):
-                nc.tensor.matmul_mx(out=idle[:], lhsT=w2h[:, 0, 0:P].bitcast(FP8X4), lhsT_scale=s2h[:, 0, 0:P],
-                                    rhs=codes[:, 0:H].bitcast(FP8X4), rhs_scale=scales[:, 0:H],
-                                    start=(i == 0), stop=(i == passes - 1))
-
         sides = (slice(0, T // 2), slice(T // 2, T))
-        warm_up("s0", 1)
-        warm_up("c1", 1)
         picked0 = plain(0, 0)
         picked1 = [plain(1, TOP - 1, None, sides[0])]
         sum0 = [bank_tile(tag, [P, T // 2], f"sum0_{tag}")[:] for tag in ("c2", "c0")]
@@ -378,7 +369,6 @@ def tile_moe_hot_mlp_relu_kernel(
             nc.scalar.copy(sum0_sb[:, cols], sum0[side])
         picked1.append(plain(1, TOP - 1, "prod0_3_0", sides[1]))
         picked2 = plain(1, TOP - 2, f"prod0_3_{T // 2}")
-        warm_up("c2", 2)
         back0 = bank_tile("s2", [P, T], "back0")[:]
         sum1 = [bank_tile(tag, [P, T // 2], f"sum1_{tag}")[:] for tag in ("c2", "s1")]
         back1 = [bank_tile(tag, [P, T // 2], f"back1_{tag}")[:] for tag in ("t0", "t1")]

from contextlib import ExitStack

import concourse.mybir as mybir
from concourse.masks import make_identity

K, T, E, C, H, N, HOT, TOP = 1024, 512, 8, 256, 512, 256, 4, 4
S = E * C
P = 128
UNITS = S // P
BLOCKS = T // P
ORDER = (0, 1, 3, 4, 5, 6, 7, 2)
XS_WIDTH = 768
HELD = {1: "c0", 2: "c2"}
SLOTS = 7
FLOPS = 2 * S * (K * H + H * N)

F32 = mybir.dt.float32
BF16 = mybir.dt.bfloat16
I32 = mybir.dt.int32
U32 = mybir.dt.uint32
U16 = mybir.dt.uint16
U8 = mybir.dt.uint8
FP8X4 = mybir.dt.float8_e4m3fn_x4
FP4X4 = mybir.dt.float4_e2m1fn_x4
RELU = mybir.ActivationFunctionType.Relu
COPY = mybir.ActivationFunctionType.Copy
MULT = mybir.AluOpType.mult
ADD = mybir.AluOpType.add


def tile_moe_hot_mlp_relu_kernel(
    tc, x_words, x_scales, w1h_words, w1h_scales, w2h_words, w2h_scales,
    w1c_words, w1c_scales, w2c_words, w2c_scales, gate, offs, pos1, pos2, pos3, pos4, out,
):
    nc = tc.nc
    with ExitStack() as ctx:
        lists = ctx.enter_context(tc.tile_pool(name="lists", bufs=1))
        keep = ctx.enter_context(tc.tile_pool(name="keep", bufs=1))
        psum = ctx.enter_context(tc.psum_pool(name="psum", bufs=1))

        def bank_tile(tag, shape, name):
            return psum.tile(shape, F32, name=name, tag=tag)

        def kept(shape, dtype, name, tag=None):
            return keep.tile(shape, dtype, name=name, tag=tag or name, align_bytes=64)

        def expert(place):
            return ORDER[place]

        def first_slot(unit):
            return ORDER[unit // 2] * C + unit % 2 * P

        def entries(unit, count):
            return offs_t[:, first_slot(unit) // 16:(first_slot(unit) + count * P) // 16]

        scale_groups = [(0, 4), (4, 2), (6, 2), (8, 2), (10, 2), (12, 2), (14, 2)]

        offs_t = lists.tile([P, S // 16], U16, name="offs_t")
        pos_t = [lists.tile([P, T // 16], U16, name=f"pos_t{r}") for r in range(TOP)]
        xw = kept([P, 2 * T], U32, "xw")
        xs = kept([P, XS_WIDTH], U8, "xs")
        w1h = {e: kept([P, 2, H], U32, f"w1h{e}") for e in ORDER[:3]}
        w1c = [kept([P, 4, 2 * H], U8, f"w1c{g}") for g in range((E - HOT) // 2)]
        s1h = [kept([P, H], U8, f"s1h{g}") for g in range(HOT // 2)]
        s1c = kept([P, 2 * (E - HOT), H], U8, "s1c")
        s2h = kept([P, HOT, N], U8, "s2h")
        s2c = kept([P, E - HOT, N], U8, "s2c")
        moved = kept([P, (E - HOT) * C], U8, "moved")
        ident0 = kept([P, P], F32, "ident0")
        ident = kept([P, P], F32, "ident")

        def as_words(tile3):
            return tile3[:].rearrange("p a b -> p (a b)").bitcast(I32)

        nc.vector.memset(xs[:].bitcast(I32), 0)
        nc.vector.memset(s1h[0][:].bitcast(I32), 0)
        nc.vector.memset(as_words(s1c), 0)
        nc.vector.memset(moved[:].bitcast(I32), 0)
        nc.vector.memset(s1h[1][:].bitcast(I32), 0)
        make_identity(nc, ident0[:])
        nc.scalar.activation(ident[:], ident0[:], RELU)
        for plane in (s2h, s2c):
            nc.vector.memset(as_words(plane), 0)

        def load_planes(tile3, scales, queue):
            src = scales.bitcast(I32).rearrange("e s (q r) n -> r q (e s) n", r=4)
            dst = tile3[:].bitcast(I32)
            for r in range(4):
                queue.dma_start(out=dst[r:P:32], in_=src[r])

        def load_w1h(e, queue=nc.sync):
            queue.dma_start(out=w1h[e][:].bitcast(I32),
                              in_=w1h_words[e].rearrange("s p i d -> p s (i d)").bitcast(I32))

        def load_w1c(g):
            nc.sync.dma_start(out=w1c[g][:].bitcast(I32),
                              in_=w1c_words[2 * g:2 * g + 2].rearrange("e s p b -> p (e s) b").bitcast(I32))

        s1h_src = w1h_scales.bitcast(I32).rearrange("(g a) s b n -> g (a s) b n", a=2)

        def load_packed(g):
            for q in range(4):
                nc.sync.dma_start(out=s1h[g][:].bitcast(I32)[32 * q:32 * q + 16],
                                  in_=s1h_src[g, :, 4 * q:4 * q + 4, :])

        def load_xw(s):
            nc.sync.dma_start(out=xw[:, s * T:(s + 1) * T].bitcast(I32),
                              in_=x_words[s].rearrange("p t d -> p (t d)").bitcast(I32))

        def load_xs():
            for q in range(4):
                nc.sync.dma_start(out=xs[:, 0:T].bitcast(I32)[32 * q:32 * q + 8],
                                  in_=x_scales.bitcast(I32)[:, 4 * q:4 * q + 4, :])

        load_xw(0)
        nc.sync.dma_start(offs_t[:], offs)
        load_xs()
        load_xw(1)
        load_w1h(0)
        load_packed(0)
        load_w1h(1)
        load_w1h(ORDER[2])
        load_packed(1)
        load_planes(s1c, w1c_scales, nc.gpsimd)
        w1h[ORDER[-1]] = kept([P, 2, H], U32, "w1h_last", "ident0")
        load_w1h(ORDER[-1], nc.gpsimd)

        ring = [(-1, f"slot{slot}") for slot in range(SLOTS)]
        ring.extend((2 * place + 1, f"w1h{ORDER[place]}") for place in range(3))
        slot_of = {}

        def gathered(shape, dtype, name, last_unit):
            taken = min(ring)
            ring.remove(taken)
            ring.append((last_unit, taken[1]))
            slot_of[name] = taken[1]
            return kept(shape, dtype, name, slot_of[name])

        gw, gs = {}, {}

        def gather_words(unit, count, s, wide=False):
            tile = gathered([P, count * P], U32, f"gw{unit}_{s}", unit + count - 1)
            window = xw[:] if wide else xw[:, s * T:(s + 1) * T]
            nc.vector.tensor_copy(tile[:], window.indirect(entries(unit, count)))
            for j in range(count):
                gw[unit + j, s] = tile[:, j * P:(j + 1) * P]

        def gather_scales(group):
            unit, count = scale_groups[group]
            tile = gathered([P, count * P], U8, f"gs{group}", unit + count - 1)
            nc.vector.tensor_copy(tile[:], xs[:].indirect(entries(unit, count)))
            for j in range(count):
                gs[unit + j] = (tile, slice(j * P, (j + 1) * P))
            cold = [u for u in range(unit, unit + count) if expert(u // 2) >= HOT]
            if cold:
                at = first_slot(cold[0]) - HOT * C
                nc.sync.dma_start(out=moved[:, at:at + len(cold) * P].bitcast(I32)[0:112],
                                  in_=tile[:, (cold[0] - unit) * P:(cold[-1] + 1 - unit) * P].bitcast(I32)[4:116])

        first_words = kept([P, P], U32, "first_words")
        nc.vector.tensor_copy(first_words[:], xw[:, 0:T].indirect(entries(0, 1)))
        gw[0, 0] = first_words[:]
        gather_words(1, 1, 0)
        gather_scales(0)
        load_w1c(0)
        gather_scales(2)
        gather_words(0, 1, 1)
        gather_words(1, 1, 1)
        gather_words(2, 2, 0, wide=True)
        gather_words(2, 2, 1)
        for place in range(2, 6):
            gather_scales(1 if place == 2 else place)
            if place == 3:
                load_w1c(1)
            gather_words(2 * place, 2, 0)
            gather_words(2 * place, 2, 1)
        gather_words(12, 2, 0)
        gather_words(12, 2, 1)
        gather_scales(6)
        for unit in (14, 15):
            gather_words(unit, 1, 0)
            gather_words(unit, 1, 1)

        w2h = kept([P, HOT, N], U32, "w2h")
        nc.sync.dma_start(out=w2h[:].bitcast(I32),
                          in_=w2h_words.rearrange("e s p n d -> p (e s) (n d)").bitcast(I32))
        load_planes(s2h, w2h_scales, nc.sync)
        w2c = kept([P, E - HOT, 2 * N], U8, "w2c")
        nc.sync.dma_start(out=w2c[:].bitcast(I32),
                          in_=w2c_words.rearrange("e s p b -> p (e s) b").bitcast(I32))
        load_planes(s2c, w2c_scales, nc.gpsimd)
        for r, pos in enumerate((pos1, pos2, pos3, pos4)):
            nc.sync.dma_start(pos_t[r][:], pos)
        gates = kept([P, TOP, T], F32, "gates")
        nc.sync.dma_start(out=gates[:], in_=gate.rearrange("r p t -> p r t"))

        last = ORDER[-1]
        w1p = kept([P, 2, H], U32, "w1p")
        s1p = kept([P, H], U8, "s1p")
        nc.gpsimd.tensor_copy(s1p[:].rearrange("p (t a b) -> p a t b", t=4, b=16),
                              s1h[last // 2][:].rearrange("p (a b t) -> p a t b", t=4, b=16))
        for s in range(2):
            nc.gpsimd.tensor_copy(w1p[:, s, :].rearrange("p (t a b) -> p a t b", t=4, b=4),
                                  w1h[last][:, s, :].rearrange("p (a b t) -> p a t b", t=4, b=4))

        hb, sums, turned_h = {}, {}, {}
        y = [kept([P, S], F32, f"y{half}") for half in range(2)]

        def layer1(unit):
            e = expert(unit // 2)
            tag = HELD.get(unit // 2 - 1) if unit % 2 == 0 else None
            sums[unit] = bank_tile(tag or f"s{unit % 3}", [P, H], f"sums{unit}")
            tile, cols = gs[unit]
            for s in range(2):
                if e < HOT:
                    w, ws = w1h[e][:, s, :].bitcast(FP8X4), s1h[e // 2][4 * (2 * (e % 2) + s):P]
                    ts = tile[4 * s:P, cols]
                else:
                    w = w1c[(e - HOT) // 2][:, 2 * (e % 2) + s, :].bitcast(FP4X4)
                    ws = s1c[:, 2 * (e - HOT) + s, :]
                    at = first_slot(unit) - HOT * C
                    ts = tile[:, cols] if s == 0 else moved[:, at:at + P]
                nc.tensor.matmul_mx(out=sums[unit][:], lhsT=gw[unit, s].bitcast(FP8X4),
                                    lhsT_scale=ts, rhs=w, rhs_scale=ws,
                                    start=(s == 0), stop=(s == 1))

        def relu(unit):
            hb[unit] = kept([P, H], BF16, f"hb{unit}")
            dst = hb[unit][:].rearrange("m (u p d) -> m u p d", u=2, d=2)
            src = sums[unit][:].rearrange("m (p u d) -> m u p d", u=2, d=2)
            nc.scalar.activation(dst, src, RELU)

        def turn_units(group):
            return [2 * group, 2 * group + 1]

        def turn(group):
            units = turn_units(group)
            if group in HELD:
                tag = HELD[group]
            else:
                tag = f"t{group % 2}"
            bank = bank_tile(tag, [P, len(units), 2, P], f"turned_h{group}")
            for i, unit in enumerate(units):
                for u in range(2):
                    nc.tensor.transpose(bank[:, i, u, :],
                                        hb[unit][:].bitcast(F32)[:, u * P:(u + 1) * P], ident[:])
            turned_h[group] = bank

        runs = [(0, 8), (8, 4), (12, 2), (14, 1), (15, 1)]
        hq = [kept([P, count, H], BF16, f"hq{first}") for first, count in runs]

        def interleave(group, copy):
            units = turn_units(group)
            run = max(i for i, (first, count) in enumerate(runs) if first <= units[0])
            at = units[0] - runs[run][0]
            dst = hq[run][:, at:at + len(units), :].bitcast(F32).rearrange("p j (m u) -> p j m u", u=2)
            copy(dst, turned_h[group][:].rearrange("p j u m -> p j m u"))

        def layer1_direct(unit):
            acc = bank_tile(f"s{unit % 3}", [P, 4, P], f"sums{unit}")
            tile, cols = gs[unit]
            for s in range(2):
                for t in range(4):
                    rows = slice(t * P, (t + 1) * P)
                    nc.tensor.matmul_mx(out=acc[:, t, :], lhsT=w1p[:, s, rows].bitcast(FP8X4),
                                        lhsT_scale=s1p[4 * s:P, rows],
                                        rhs=gw[unit, s].bitcast(FP8X4), rhs_scale=tile[4 * s:P, cols],
                                        start=(s == 0 and t == 0), stop=(s == 1 and t == 3))
            dst = hq[unit - UNITS + len(runs)][:, 0, :].rearrange("p (m t) -> p m t", t=4)
            nc.scalar.activation(dst, acc[:].rearrange("p t m -> p m t"), RELU)

        for place in range(E - 1):
            for unit in (2 * place, 2 * place + 1):
                layer1(unit)
                relu(unit)
            if place >= 1:
                turn(place - 1)
                interleave(place - 1, nc.scalar.copy)
        layer1_direct(UNITS - 2)
        turn(E - 2)
        interleave(E - 2, nc.scalar.copy)
        layer1_direct(UNITS - 1)

        codes = kept([P, S], U32, "codes", slot_of["gs5"])
        scales = kept([P, S], U8, "scales")

        def quantise(run):
            first, count = runs[run]
            cols = slice(first * P, (first + count) * P)
            nc.vector.quantize_mx(out=codes[:, cols].bitcast(FP8X4), scales=scales[:, cols],
                                  in_=hq[run][:].rearrange("p a c -> p (a c)"))

        outs = {}

        def layer2(places, half, tag):
            acc = bank_tile(tag, [P, len(places), C], f"y{half}_{places[0]}")
            cols = slice(half * P, (half + 1) * P)
            for j, place in enumerate(places):
                e = expert(place)
                if e < HOT:
                    w, ws = w2h[:, e, cols].bitcast(FP8X4), s2h[:, e, cols]
                else:
                    w = w2c[:, e - HOT, 2 * half * P:2 * (half + 1) * P].bitcast(FP4X4)
                    ws = s2c[:, e - HOT, cols]
                slots = slice(place * C, (place + 1) * C)
                nc.tensor.matmul_mx(out=acc[:, j, :], lhsT=w, lhsT_scale=ws,
                                    rhs=codes[:, slots].bitcast(FP8X4), rhs_scale=scales[:, slots],
                                    start=True, stop=True)
            outs[places[0], half] = acc

        def results(places, half, copy):
            first, last = expert(places[0]), expert(places[-1])
            by_expert = y[half][:].rearrange("p (e c) -> p e c", c=C)
            copy(by_expert[:, first:last + 1:max(last - first, 1), :], outs[places[0], half][:])

        for run in range(len(runs)):
            quantise(run)
        layer2([0, 1], 0, "s1")
        results([0, 1], 0, nc.scalar.copy)
        layer2([2, 3], 0, "s2")
        results([2, 3], 0, nc.scalar.copy)
        layer2([4, 5], 0, "s0")
        results([4, 5], 0, nc.scalar.copy)
        layer2([6], 0, "c0")
        results([6], 0, nc.vector.tensor_copy)
        layer2([7], 0, "c1")
        results([7], 0, nc.vector.tensor_copy)

        def fused(half, r, cols=slice(0, T)):
            product = kept([P, cols.stop - cols.start], F32, f"prod{half}_{r}_{cols.start}")
            nc.vector.tensor_tensor(product[:], y[half][:].indirect(pos_t[r][:, cols.start // 16:cols.stop // 16]),
                                    gates[:, r, cols], MULT)
            return product

        def plain(half, r, tag=None, cols=slice(0, T)):
            picked = kept([P, cols.stop - cols.start], F32, f"pick{half}_{r}_{cols.start}", tag)
            nc.scalar.activation(picked[:], y[half][:].indirect(pos_t[r][:, cols.start // 16:cols.stop // 16]), COPY)
            return picked

        def turn_into(acc, src, first, last):
            blocks = src.shape[1] // P
            for c in range(blocks):
                cols = slice(c * P, (c + 1) * P)
                nc.tensor.matmul(acc[:, cols], lhsT=src[:, cols], rhs=ident[:], is_transpose=True,
                                 start=(first and c == 0), stop=(last and c == blocks - 1))

        for pair, tag in ((0, "s1"), (2, "s2"), (3, "s0"), (1, "c1")):
            places = [ORDER.index(2 * pair), ORDER.index(2 * pair + 1)]
            layer2(places, 1, tag)
            results(places, 1, nc.scalar.copy)

        def gated(picked, half, r, cols=slice(0, T)):
            product = kept([P, cols.stop - cols.start], F32, f"prod{half}_{r}_{cols.start}")
            nc.vector.tensor_tensor(product[:], picked[:, cols], gates[:, r, cols], MULT)
            return product

        sides = (slice(0, T // 2), slice(T // 2, T))
        picked0 = plain(0, 0)
        picked1 = [plain(1, TOP - 1, None, sides[0])]
        sum0 = [bank_tile(tag, [P, T // 2], f"sum0_{tag}")[:] for tag in ("c2", "c0")]
        for r in range(1, TOP - 1):
            product = fused(0, r)
            for side, cols in enumerate(sides):
                turn_into(sum0[side], product[:, cols], r == 1, False)
        for side, cols in enumerate(sides):
            turn_into(sum0[side], fused(0, TOP - 1, cols)[:], False, True)
        sum0_sb = kept([P, T], F32, "sum0_sb")
        for side, cols in enumerate(sides):
            nc.scalar.copy(sum0_sb[:, cols], sum0[side])
        picked1.append(plain(1, TOP - 1, "prod0_3_0", sides[1]))
        picked2 = plain(1, TOP - 2, f"prod0_3_{T // 2}")
        back0 = bank_tile("s2", [P, T], "back0")[:]
        sum1 = [bank_tile(tag, [P, T // 2], f"sum1_{tag}")[:] for tag in ("c2", "s1")]
        back1 = [bank_tile(tag, [P, T // 2], f"back1_{tag}")[:] for tag in ("t0", "t1")]

        product = fused(1, 0)
        for side, cols in enumerate(sides):
            turn_into(sum1[side], product[:, cols], True, False)
        turn_into(back0, sum0_sb[:], True, True)
        for side, cols in enumerate(sides):
            product = kept([P, T // 2], F32, f"prod1_3_{side}")
            nc.vector.tensor_tensor(product[:], picked1[side][:], gates[:, TOP - 1, cols], MULT)
            turn_into(sum1[side], product[:], False, False)
            turn_into(sum1[side], fused(1, 1, cols)[:], False, True)
        for side in range(2):
            sum1_sb = kept([P, T // 2], F32, f"sum1_sb{side}")
            nc.scalar.copy(sum1_sb[:], sum1[side])
            turn_into(back1[side], sum1_sb[:], True, True)
        rest0 = kept([P, T], F32, "rest0", "prod0_3_0")
        for cols in sides:
            nc.vector.tensor_tensor(rest0[:, cols], picked0[:, cols], gates[:, 0, cols], MULT)
        res0 = kept([P, T], F32, "res0")
        for side, cols in enumerate(sides):
            nc.vector.tensor_tensor(res0[:, cols], back0[:, cols], rest0[:, cols], ADD)
        nc.sync.dma_start(out=out[0:P, :], in_=res0[:])
        rest1 = [gated(picked2, 1, TOP - 2, cols) for cols in sides]
        for side, cols in enumerate(sides):
            res = kept([P, T // 2], F32, f"res1_{side}")
            nc.vector.tensor_tensor(res[:], back1[side], rest1[side][:], ADD)
            nc.sync.dma_start(out=out[P:2 * P, cols], in_=res[:])
